import numpy as np, ml_dtypes
CORES = [66,74,82,90,194,202,210,218]
N = 8
BF = ml_dtypes.bfloat16
def gentries(a):
    return np.ascontiguousarray(a.reshape(8, 16, -1).transpose(0, 2, 1)).reshape(8, -1)
def gtable(e):
    e = np.asarray(e); return np.ascontiguousarray(e.reshape(8, -1, 16).transpose(0, 2, 1)).reshape(128, -1).astype(np.int32)
L, K, B, RO, CAP = 1792, 896, 2, 10, 96
R = RO // B - 1
def pick(a, v):
    return np.take_along_axis(a, v[:, :, None, :], 3)
def moved(p, c):
    q = p + np.sum(c, axis=2)
    return np.where(q >= 16 * L, q - 16 * L, q)
def sums(C):
    return np.sum(C[..., B - 1::B], axis=2)
def splice(a, cut):
    ids = np.argsort(~cut, axis=2, kind="stable"); n = np.minimum(np.add.reduce(cut.astype(np.int64), axis=2), CAP)
    old = a.reshape(N, 8, 16, K, B); new = old.copy()
    for r in range(N):
        q = (r - 1) % N
        for g in range(8):
            m = min(int(n[r, g]), int(n[q, g]))
            new[r, g][:, ids[r, g, :m]] = old[q, g][:, ids[q, g, :m]]
    return new.reshape(N, 8, 16, L)
def parts(rng):
    x = np.abs(rng.standard_normal((N, 128, L), dtype=np.float32)) * np.exp2(rng.integers(-1, 2, (N, 128, 1)))
    return x, rng.integers(0, 16, (N, 8, 16, L)), rng.integers(0, 16 * L, (N, 8, K)), rng.integers(100, 170, (N, 8, R))
def pack(x, C, p, th):
    return {"tape": np.clip(x, 0, 4).astype(np.float32).astype(BF), "ctl": np.ascontiguousarray(C.reshape(N, 128, L)).astype(np.float32).astype(BF),
            "pos": np.stack([gtable(a) for a in p]), "th": th.astype(np.int32)}
def cols(rng, s):
    c = (s >> 4)[None, :] + (np.argsort(rng.random((16, len(s))), axis=0) < (s & 15)[None, :])
    d = (rng.random((8, len(s))) * (np.minimum(c[0::2], 15 - c[1::2]) + 1)).astype(np.int64)
    c[0::2] -= d; c[1::2] += d
    return c
def tuned(p, C, want):
    C = C.copy(); th = np.zeros((N, 8, R), np.int64)
    for t in range(RO - B):
        j = t % B; c = pick(C, p >> 4)
        C[..., j::B] = (c + C[..., j::B]) & 15
        p = moved(p, c)
        if j == B - 1:
            m = t // B; S = sums(C); D = -np.sort(-S, axis=2); w = want[m]
            a = np.take_along_axis(D, np.maximum(w - 1, 0)[..., None], 2)[..., 0]
            th[:, :, m] = np.where(w == 0, np.minimum(D[..., 0] + 1, 240), a)
            C = splice(C, S >= th[:, :, m, None])
    return th
def setup_inputs(rng):
    x, C, p, th = parts(rng); u = rng.random((N, 8, 1, L))
    C = np.where(u < 0.04, 0, np.where(u > 0.97, 15, C))
    p[..., K - 1] = 16 * L - 1; p[..., 0] = 16 * (L - 1) + rng.integers(0, 16, (N, 8))
    return pack(x, C, p, th)
def setup_inputs_spread(rng):
    x, C, p, th = parts(rng)
    x = x * np.exp2(rng.integers(-3, 4, (N, 1, L))) * (rng.random((N, 1, L)) > 0.0625)
    e = rng.choice(np.array([0.3, 1.0, 3.0]), (N, 8, 1, L), p=np.array([0.25, 0.5, 0.25]))
    C = np.minimum((16 * rng.random((N, 8, 16, L)) ** e).astype(np.int64), 15)
    p = np.where(rng.random((N, 8, K)) < 0.5, p, np.minimum((16 * L * rng.random((N, 8, K)) ** 3).astype(np.int64), 16 * L - 1))
    return pack(x, C, p, rng.integers(40, 200, (N, 8, R)))
def setup_inputs_ends(rng):
    x, C, p, th = parts(rng)
    x = np.where(rng.random(x.shape) < 0.7, np.where(rng.random(x.shape) < 0.5, 0.0, 4.0), x)
    u = rng.random((N, 8, 1, L)); C = np.where(u < 0.3, 0, np.where(u < 0.6, 15, 15 * rng.integers(0, 2, C.shape)))
    p = np.where(rng.random(p.shape) < 0.68, (16 * L - 1) * rng.integers(0, 2, p.shape), p)
    th = np.where(rng.random(th.shape) < 0.85, 240 * rng.integers(0, 2, th.shape), th)
    th[:, :, 0] = 240 * rng.integers(0, 2, (N, 8)); th[:, 0, 0] = 0; th[:, 1, 0] = 240; th[N - 1, 7, 0] = 240; th[0, 7, 0] = 240
    few = np.array([0, 1, 2, 3, K - 2, K - 1]); z = (K // 2) * B + B - 1
    for r in range(N):
        for g in range(8):
            o = (g + r) % 4
            if o == 3: continue
            C[r, g][:, z] = 0; C[r, g][:, few * B + B - 1] = 0 if o == 1 else 15
            p[r, g, few] = 16 * z + rng.integers(0, 16, len(few)); p[r, g, 4] = 0; p[r, g, K - 3] = 16 * L - 1
            if o == 1 and g > 3: th[r, g, 0] = 1
    return pack(x, C, p, th)
def setup_inputs_corners(rng):
    x, C, p, th = parts(rng)
    a = C.copy(); q = p; seen = np.zeros((N, 8, L), bool)
    for t in range(B):
        v = q >> 4; np.put_along_axis(seen, v, True, 2); c = pick(a, v)
        if t < B - 1:
            a[..., t::B] = (c + a[..., t::B]) & 15
            q = moved(q, c)
    free = ~seen[..., B - 1::B]; S = np.sum((c + C[..., B - 1::B]) & 15, axis=2)
    few = [CAP, CAP + 1, 0, CAP - 1, 1, K - 1, 2, K, 3, 256, 255]; o = int(rng.integers(0, 11))
    for r in range(N):
        for g in range(8):
            e = np.flatnonzero(free[r, g]); e = np.concatenate([e[-1:], e[:1], rng.permutation(e[1:-1])]); b = S[r, g][~free[r, g]]
            n = few[((r // 2 if g % 2 == 1 else r) + 3 * g + o) % 11]
            if n >= K - 1: lo = int(np.min(b)); m = len(e) - (K - n)
            else: lo = int(np.max(b)) + 1; m = n
            lo = min(max(lo, 1), 240); coin = rng.random(len(e)) < 0.5
            s = np.where(np.arange(len(e)) < m, np.where(coin, lo, rng.integers(lo, 241, len(e))), np.where(coin, lo - 1, rng.integers(0, lo, len(e))))
            C[r, g][:, e * B + B - 1] = (cols(rng, s) - c[r, g][:, e]) & 15
            th[r, g, 0] = lo
    th[:, 2, 1] = 240; th[:, 6, 1] = 240
    return pack(x, C, p, th)
def setup_inputs_crowd(rng):
    x, C, p, th = parts(rng)
    for r in range(N):
        for g in range(8):
            o = (g + r) % 4; at = int(rng.integers(0, 16 * L))
            if o < 2: p[r, g] = at
            if o == 1: p[r, g, K - 1] = (at + 8 * L) % (16 * L)
            if o == 2:
                own = 16 * B * np.arange(K) + rng.integers(0, 16 * B, K)
                p[r, g] = np.where(rng.random(K) < 0.5, own, rng.choice(np.array([0, 15, 16 * L - 1, 16 * (L - 1), at]), K))
            if o == 3:
                s = int(rng.integers(2, 16)); C[r, g][:, 0] = 0; C[r, g][:, B - 1] = 0; C[r, g][:, L - 1] = cols(rng, np.array([s]))[:, 0]
                p[r, g, 0] = int(rng.integers(0, 16)); p[r, g, np.array([1, K // 2, K - 1])] = 16 * L - s; p[r, g, 2] = 16 * L - s + 1; p[r, g, 3] = 16 * L - s - 1
    return pack(x, C, p, th)
def setup_inputs_calm(rng):
    x, C, p, th = parts(rng)
    for r in range(N):
        C[r, 0] = cols(rng, rng.integers(0, 4, L)); p[r, 0] = (p[r, 0] & -16) + 15 - rng.integers(0, 4, K)
        C[r, 4] = 0; C[r, 4][:, B - 1::B] = cols(rng, rng.integers(0, 4, K))
        p[r, 4] = 16 * (B * rng.integers(0, K, K) + rng.integers(0, B - 1, K)) + rng.integers(0, 16, K)
        for g in (2, 6): C[r, g] = cols(rng, rng.choice(np.array([0, 239, 240]), L))
    few = np.array([1, 0, 2, K - 1, 3, K, CAP, CAP + 1])
    o = np.arange(R)[:, None, None] + np.arange(N)[None, :, None] + 3 * np.arange(8)[None, None, :] + int(rng.integers(0, 8))
    th = tuned(p, C, few[o % 8])
    th[:, 4] = 1 + (np.arange(N)[:, None] + np.arange(R)[None, :] + int(rng.integers(0, 3))) % 3
    return pack(x, C, p, th)
def check_ranges(d):
    bad = []
    for k, lo, hi in (("tape", 0, 4), ("ctl", 0, 15), ("pos", 0, 16 * L - 1), ("th", 0, 240)):
        a = np.asarray(d[k]).astype(np.float64)
        if not (np.min(a) >= lo and np.max(a) <= hi): bad.append("range of " + k)
        elif k == "ctl" and not np.all(a == np.floor(a)): bad.append("whole numbers of ctl")
    return bad
def reference(tape, ctl, pos, th):
    X = tape.astype(np.float64).reshape(N, 8, 16, L); C = ctl.astype(np.float32).astype(np.int64).reshape(N, 8, 16, L)
    p = np.stack([gentries(a) for a in pos]).astype(np.int64); late = np.zeros((N, 8, 16, K))
    for t in range(RO):
        j = t % B; v = p >> 4; w = np.where(v == L - 1, 0, v + 1); part = ((p & 15) * 0.0625)[:, :, None, :]
        a = pick(X, v); s = a + part * (pick(X, w) - a); c = pick(C, v)
        if t > 0: late = np.roll(np.roll(before, 1, axis=0), -t, axis=1)
        X[..., j::B] = np.tanh(0.625 * s + 0.375 * late)
        C[..., j::B] = (c + C[..., j::B]) & 15
        p = moved(p, c); before = s
        if j == B - 1 and t < RO - 1:
            cut = sums(C) >= th[:, :, t // B].astype(np.int64)[:, :, None]
            X = splice(X, cut); C = splice(C, cut)
    return {"yx": X.reshape(N, 128, L).astype(np.float32), "yc": np.sum(C, axis=2).astype(np.float32),
            "yp": np.stack([np.concatenate([gtable(a >> 8), gtable(a & 255)], axis=1) for a in p]).astype(np.float32)}

def check_inputs(d):
    bad = list(check_ranges(d))
    if not bad:
        for name, y in reference(**d).items():
            for q in range(N):
                v = np.abs(np.asarray(y[q], np.float64)); s = np.sqrt(np.mean(v * v))
                if v.max() > 4 * s or s < 2.0 ** -3: bad.append('%s of rank %d is uneven or too small' % (name, q))
    return bad

@@ -1,0 +1,687 @@
+import numpy as np
+from concourse.bass import DstId, RemoteDMATransfer
+from concourse.mybir import AluOpType, ActivationFunctionType
+
+A = AluOpType
+F = ActivationFunctionType
+L, K, H, STEPS, NR, CAP, WORLD = 1792, 896, 448, 10, 4, 96, 256
+XW = L + 2 + 2 * CAP
+RING = 16 * L
+PW, PC = 204, 208
+
+CH = [(0, 28, "pE0", 0, "pA0", 0), (28, 56, "pE1", 0, "pA1", 0)]
+ROUTE = {0: [["A0", "B0"], ["D"]], 1: [["A0", "B0"], ["A1", "B1"]]}
+ZLAST = {0: [False] * 4, 1: [True] * 4}
+XEARLY = True
+CG0, CG = "av", {0: "aa", 1: "aa"}
+DN = {0: "vv", 1: "vv"}
+ADD = {0: "pv", 1: "pv"}
+LATE = {}
+CODE = {}
+SLACK, LEAD, AHEAD = 0.15, 1.0, 2.0
+SHIFT = {'c0': 'QMMMKNOLQKMMMJQIJHIN', 'c1': 'MMMMMMMQRMMMQOMMMRMMMJMPHIMKNLMMMMMMMMTLQMJMNPQ', 'e': 'MSMMIMOP',
+         'i': 'MONMOKMPMKMTOMMMMQMMMMMMMINUMMPPMMMLNMMNMQMQILMNM', 'x0': 'MMMPMKMOKOMOMQMMKKMM', 'x1': 'IQMMLGMOMMLNNLJMIIMKMMOIMM',
+         'xa': 'QHNMLNQMMRRLMMM', 'xb': 'MMKMMMMMMMMLMMMMKIM'}
+MODEL = dict(cy=0.001, py=0.0005, fix=0.06, g=1.55, t=1.8, s=3.5, sem=0.1, issue=0.6, up=2.0, link=60e3, chip=120e3, eng=15e3, hbm=200e3)
+SPREAD = [{}, dict(py=0.00075, g=1.2, t=1.2, s=2.0, sem=0.15, issue=0.9, up=2.6, link=45e3, eng=11e3),
+          dict(cy=0.00115, py=0.00058, g=1.9, t=2.0, s=5.0, sem=0.07, issue=0.4, up=1.5, link=100e3, eng=20e3)]
+ROUNDS, HEAT = 8000, 0.3
+
+SCRATCH = {
+    "rawx": ("sbuf", [128, L + 16], "bfloat16"), "rawc": ("sbuf", [128, L], "bfloat16"),
+    "X": ("sbuf", [128, XW + 6], "float32"), "D": ("sbuf", [128, XW + 6], "bfloat16"),
+    "posi": ("sbuf", [128, 56], "int32"), "P": ("sbuf", [128, 56], "float32"), "wr": ("sbuf", [128, 56], "float32"),
+    "Pi": ("sbuf", [128, 56], "int32"), "fr": ("sbuf", [128, 56], "int32"),
+    "offv": ("sbuf", [128, 560], "uint16"), "offw": ("sbuf", [128, 560], "uint16"), "phi": ("sbuf", [128, 1120], "bfloat16"),
+    "cg": ("sbuf", [128, K], "bfloat16"), "sg": ("sbuf", [128, K], "bfloat16"),
+    "a": ("sbuf", [128, K], "float32"), "d": ("sbuf", [128, K], "float32"),
+    "s": ("sbuf", [128, K * STEPS], "float32"), "zl": ("sbuf", [128, K * (STEPS - 1)], "float32"),
+    "s16": ("sbuf", [128, K * (STEPS - 1)], "uint16"), "z16": ("sbuf", [128, K * (STEPS - 1)], "uint16"),
+    "pc": ("sbuf", [128, PC * NR], "bfloat16"), "lc": ("sbuf", [128, PC * NR], "bfloat16"),
+    "px": ("sbuf", [128, 192 * NR], "float32"), "lx": ("sbuf", [128, 192 * NR], "float32"),
+    "srcl": ("sbuf", [128, 12 * NR], "uint16"), "dstl": ("sbuf", [128, 12 * NR], "uint16"),
+    "cut": ("sbuf", [128, 56], "bfloat16"), "Tc": ("sbuf", [128, 56], "float32"), "cum": ("sbuf", [128, 56], "float32"),
+    "junk": ("sbuf", [128, 336], "bfloat16"), "acc": ("sbuf", [128, 6], "float32"), "colk": ("sbuf", [128, 6], "uint16"),
+    "col32": ("sbuf", [128, 6], "float32"), "fl": ("sbuf", [128, 96], "bfloat16"),
+    "o12": ("sbuf", [128, 12], "float32"), "y12": ("sbuf", [128, 12], "float32"),
+    "thi": ("sbuf", [128, 4], "int32"), "thb": ("sbuf", [128, 4], "bfloat16"), "thc": ("sbuf", [128, 4], "float32"),
+    "ci": ("sbuf", [128, 8], "int32"), "cf": ("sbuf", [128, 12], "float32"),
+    "xr": ("sbuf", [128, 256], "float32"), "xe": ("sbuf", [128, 256], "bfloat16"),
+    "Wi": ("sbuf", [128, 256], "float32"), "Wz": ("sbuf", [128, 256], "float32"),
+    "Ib": ("sbuf", [128, 128], "bfloat16"), "W8": ("sbuf", [128, 144], "bfloat16"), "W2": ("sbuf", [128, 144], "bfloat16"),
+    "E8": ("sbuf", [128, 1024], "bfloat16"), "Bm": ("sbuf", [128, 128], "bfloat16"), "Um": ("sbuf", [128, 128], "bfloat16"),
+    "sel": ("sbuf", [128, 128], "bfloat16"), "ones": ("sbuf", [128, 56], "float32"),
+    "kcol": ("sbuf", [128, 6], "float32"), "dump": ("sbuf", [128, 12], "float32"),
+    "ypi": ("sbuf", [128, 112], "int32"), "ypf": ("sbuf", [128, 112], "float32"), "ycf": ("sbuf", [128, 112], "float32"),
+    "pE0": ("psum", [128, 512], "float32"), "pE1": ("psum", [128, 512], "float32"),
+    "pA0": ("psum", [128, 512], "float32"), "pA1": ("psum", [128, 512], "float32"),
+    "pT0": ("psum", [128, 512], "float32"), "pT1": ("psum", [128, 512], "float32"),
+    "pS": ("psum", [128, 512], "float32"), "pR": ("psum", [128, 512], "float32"),
+}
+
+
+def pieces(t):
+    out = []
+    for h, c in enumerate(CH):
+        ways = ROUTE[t % 2][h]
+        n = 16 * (c[1] - c[0]) // len(ways)
+        for i, w in enumerate(ways):
+            out.append((h, w, 16 * c[0] + i * n, n, "z%d_%d" % (t, len(out))))
+    return out
+
+
+def land(o, at, M, busy):
+    out = {}
+    for sem, w in o["ways"].items():
+        like = sum((x[0] == "A") == (w[0] == "A") for x in o["ways"].values())
+        rate, t = M["eng"] * 8 / like, at + M["up"]
+        if w != "D":
+            t += o["n"] / min(rate, M["chip"]) + M["issue"] + M["up"]
+            rate = M["eng"] * 8
+        k = w[0] if w[0] == "A" else w
+        busy[k] = max(t, busy.get(k, 0.0)) + o["n"] / M["link"]
+        out[sem] = max(busy[k], t + o["n"] / rate)
+    return out
+
+
+def cost(o, M):
+    q, n = o["q"], o["n"]
+    if "send" in o:
+        return M["issue"], 0.0
+    if q == "sync":
+        return 0.1, 2.0 + n / M["hbm"]
+    if q == "pool":
+        return 0.13 + 2 * n * M["cy"], 0.0
+    if q == "pe":
+        return M["fix"] + n * M["py"], 0.0
+    return M["fix"] + max(64, n * M.get(o["k"], o["k"])) * M["cy"], 0.0
+
+
+SEMAPHORES = (["pe", "dve", "act", "pool", "sent", "l0", "l1", "l2", "l3", "l4", "st"]
+              + [p[4] for t in range(STEPS - 1) for p in pieces(t)]
+              + ["r%s%d" % (x, m) for x in ("c", "e", "o") for m in range(NR)])
+BANKS = ("pE0", "pE1", "pA0", "pA1", "pT0", "pT1", "pS", "pR")
+
+
+def build():
+    ops, part = [], ["i", 0]
+
+    def op(q, n, rd, wr, fn, k=1.0, **kw):
+        o = dict(q=q, n=n, k=k, rd=list(rd), wr=list(wr), fn=fn, cls=(part[0], part[1]))
+        part[1] += 1
+        o.update(kw)
+        ops.append(o)
+
+    def V(n, rd, wr, fn, k=1.0):
+        op("dve", n, rd, wr, fn, k)
+
+    def S(n, rd, wr, fn, k=1.0):
+        op("act", n, rd, wr, fn, k)
+
+    def PE(cyc, rd, wr, fn):
+        op("pe", cyc, rd, wr, fn)
+
+    def ts(o, i, s1, s2, o0, o1=None):
+        if o1 is None:
+            return lambda g, T: g.vector.tensor_scalar(o(T), i(T), s1(T) if s1 is not None and not isinstance(s1, (int, float)) else s1, None, o0)
+        return lambda g, T: g.vector.tensor_scalar(o(T), i(T), s1(T) if not isinstance(s1, (int, float)) else s1,
+                                                   s2(T) if not isinstance(s2, (int, float)) else s2, o0, o1)
+
+    def tt(o, i0, i1, alu):
+        return lambda g, T: g.vector.tensor_tensor(o(T), i0(T), i1(T), alu)
+
+    def cp(o, i):
+        return lambda g, T: g.vector.tensor_copy(o(T), i(T))
+
+    def act(o, i, f, **kw):
+        return lambda g, T: g.scalar.activation(o(T), i(T), f, **kw)
+
+    def B(name, a=None, b=None, c=None):
+        return lambda T: T[name][:, a:b:c] if c else T[name][:, a:b]
+
+    def G(name, w, lst, a, b):
+        return lambda T: T[name][:, 0:w].indirect(T[lst][:, a:b])
+
+    def mms(lst):
+        def fn(g, T):
+            r = None
+            for o, l, rh, st, sp in lst:
+                r = g.tensor.matmul(o(T), l(T), rh(T), st, sp)
+            return r
+        return fn
+
+    def col(j):
+        return B("cf", j, j + 1)
+
+    def dma(q, sem, nbytes, rd, wr, fn):
+        op(q, nbytes, rd, wr, fn, sem=sem, inc=16)
+
+    XA = ["X%d%d" % (p, h) for p in range(2) for h in range(len(CH))] + ["Xm"]
+    DA = ["D00", "D01", "D10", "D11"]
+    GK = "g"
+
+    dma("sync", "l0", 0, [], ["posi"], lambda g, T: g.sync.dma_start(T.posi[:], T.pos[:]))
+    dma("sync", "l1", 460e3, [], ["rawc"], lambda g, T: g.sync.dma_start(T.rawc[:], T.ctl[:]))
+    dma("sync", "l2", 920e3, [], ["rawx"], lambda g, T: g.sync.dma_start(T.rawx[:, 0:L], T.tape[:]))
+    dma("sync", "l3", 920e3, [], ["thi"], lambda g, T: g.sync.dma_start(T.thi[0:8, :], T.th[:]))
+
+    op("pool", 1, [], ["ci0"], lambda g, T: g.iota(T.ci[:, 0:1], [[0, 1]], 0, 1))
+    op("pool", 256, [], ["xr"], lambda g, T: g.iota(T.xr[:], [[0, 2], [1, 128]], 0, 0, allow_small_or_imprecise_dtypes=True))
+    op("pool", 256, [], ["xe"], lambda g, T: g.iota(T.xe[:], [[1, 2], [16, 8], [0, 16]], 0, 0, allow_small_or_imprecise_dtypes=True))
+    for j, msk in enumerate((112, 15, 119, 8)):
+        V(1, ["ci0"], ["ci%d" % (j + 1)], ts(B("ci", j + 1, j + 2), B("ci", 0, 1), msk, None, A.bitwise_and))
+    V(5, ["ci%d" % j for j in range(5)], ["cf"], cp(B("cf", 0, 5), B("ci", 0, 5)))
+    V(1, ["cf"], ["cf5"], ts(col(5), col(1), 15.0, None, A.add))
+    V(1, ["cf"], ["cf6"], ts(col(6), col(4), 0.0, 0.0625, A.is_equal, A.mult))
+    V(1, ["cf"], ["cf7"], ts(col(7), col(4), 8.0, 0.0625, A.is_equal, A.mult))
+    V(1, ["cf"], ["cf8"], ts(col(8), col(0), 16.0, None, A.mult))
+    V(256, ["cf", "xr"], ["Wi"], ts(B("Wi"), B("xr"), col(0), None, A.is_equal))
+    S(256, ["Wi"], ["Wz"], act(B("Wz"), B("Wi"), F.Copy, scale=0.6))
+    S(128, ["Wi"], ["Ib"], act(B("Ib"), B("Wi", 0, 128), F.Copy))
+    V(144, ["cf5", "xr"], ["W8"], ts(B("W8"), B("xr", 0, 144), col(5), 8.0, A.is_equal, A.mult))
+    S(144, ["W8"], ["W2"], act(B("W2"), B("W8"), F.Copy, scale=0.25))
+    for j in range(4):
+        V(256, ["cf", "xe"] + ["E8"] * (j == 3), ["E8"] if j == 3 else ["E8_%d" % j],
+          ts(B("E8", 256 * j, 256 * j + 256), B("xe"), 2.0 * j, col(3), A.add, A.is_equal), 0.5)
+    ops[-1]["rd"] = ["cf", "xe", "E8_0", "E8_1", "E8_2"]
+    V(128, ["cf", "xe"], ["Bm"], ts(B("Bm"), B("xe", 0, 128), col(1), None, A.is_equal), 0.5)
+    V(128, ["cf", "xr"], ["Um"], ts(B("Um"), B("xr", 0, 128), col(0), -1.0, A.is_lt, A.mult))
+    V(128, ["Um", "Bm"], ["Um"], tt(B("Um"), B("Um"), B("Bm"), A.mult))
+    V(128, ["cf8", "xe"], ["sel"], ts(B("sel"), B("xe", 0, 128), col(8), None, A.is_equal), 0.5)
+    V(6, ["cf", "xr"], ["kcol"], ts(B("kcol"), B("xr", 0, 96, 16), col(2), 0.5, A.add, A.add))
+    for j in range(2):
+        V(6, ["kcol"], ["dump%d" % j], ts(B("dump", 6 * j, 6 * j + 6), B("kcol"), 2.0, float(L + 1 + j), A.mult, A.add))
+    V(56, [], ["ones"], lambda g, T: g.vector.memset(T.ones[:], 1.0))
+    V(100, [], ["Dd"], lambda g, T: g.vector.memset(T.D[:, L:XW], 0.0))
+    S(1500, ["xr"], ["Xd", "Xm"], act(B("X", L, XW), B("xr", 0, XW - L), F.Tanh))
+    V(4, ["thi"], ["thb"], lambda g, T: g.vector.tensor_copy(T.thb[0:8, :], T.thi[0:8, :]))
+    PE(64, ["thb", "sel"], ["pR"], lambda g, T: g.tensor.matmul(T.pR[:, 0:4], T.sel[0:8, :], T.thb[0:8, :], True, True))
+    V(4, ["pR"], ["thc"], ts(B("thc"), B("pR", 0, 4), -128.0, None, A.add))
+    V(1, ["rawx"], ["rawm"], cp(B("rawx", L, L + 1), B("rawx", 0, 1)))
+    for p in range(2):
+        V(K, ["rawc"], ["D%d0" % p, "D%d1" % p], ts(B("D", p, L, 2), B("rawc", p, L, 2), 0.125, -1.0, A.mult, A.add), 0.5)
+    for h, c in enumerate(CH):
+        S(16 * (c[1] - c[0]), ["rawx"], ["X1%d" % h], act(B("X", 1 + 32 * c[0], 32 * c[1], 2), B("rawx", 1 + 32 * c[0], 32 * c[1], 2), F.Copy))
+    V(56, ["posi"], ["P"], cp(B("P"), B("posi")))
+
+    def lists(t):
+        src, tok = (B("posi"), "posi") if t == 0 else (B("P"), "P")
+        V(56, [tok], ["offv%d" % t], ts(B("offv", 56 * t, 56 * t + 56), src, 0.0625, 8.0 * t - 0.46875, A.mult, A.add))
+        V(56, [tok], ["offw%d" % t], ts(B("offw", 56 * t, 56 * t + 56), src, 0.0625, 8.0 * t + 0.53125, A.mult, A.add))
+        if t:
+            V(56, ["P"], ["Pi"], ts(B("Pi"), B("P"), 128.0 * t, None, A.add))
+        V(56, ["Pi" if t else "posi"], ["fr"], ts(B("fr"), B("Pi") if t else B("posi"), 15, None, A.bitwise_and))
+        for j in range(2):
+            V(56, ["fr", "cf%d" % (6 + j)], ["phi%d_%d" % (t, j)], ts(B("phi", 112 * t + j, 112 * t + 112, 2), B("fr"), col(6 + j), None, A.mult))
+
+    def cstep(t):
+        par = t % 2
+        o = 56 * t
+        PE(256, ["P", "Wi"], ["pS"], mms([(B("pS", 0, 56), B("Wi", 0, 128), B("P"), True, False)]))
+        for h in range(2):
+            PE(H, ["Ib", "D%d%d" % (par, h)], ["pT%d" % h],
+               mms([(B("pT%d" % h, 0, H), B("Ib"), B("D", par + K * h, K * (h + 1), 2), True, False)]))
+        for h in range(2):
+            out, w = B("cg", H * h, H * h + H), G("D" if t else "rawc", L, "offv", o + 28 * h, o + 28 * h + 28)
+            rd = (DA if t else ["rawc"]) + ["offv%d" % t]
+            if (CG0 if t == 0 else CG[par])[h] == "a":
+                S(H, rd, ["cg%d" % h], act(out, w, F.Copy) if t else act(out, w, F.Copy, scale=0.125, bias=-1.0), "g")
+            else:
+                V(H, rd, ["cg%d" % h], cp(out, w) if t else ts(out, w, 0.125, -1.0, A.mult, A.add), "g")
+        for h in range(2):
+            PE(H, ["Ib", "cg%d" % h], ["pT%d" % h], mms([(B("pT%d" % h, 0, H), B("Ib"), B("cg", H * h, H * h + H), False, True)]))
+        PE(1024, ["W8", "cg0", "cg1"], ["pS"],
+           mms([(B("pS", 0, 56), B("W8", 15 - m, 143 - m), B("cg", m, K, 16), False, m == 15) for m in range(16)]))
+        for h in range(2):
+            pt, sh, out = B("pT%d" % h, 0, H), B("sg", H * h, H * h + H), B("D", par + K * h, K * (h + 1), 2)
+            if DN[par][h] == "v":
+                S(H, ["pT%d" % h], ["sg%d" % h], act(sh, pt, F.Sign, bias=0.0625))
+                V(H, ["pT%d" % h, "sg%d" % h], ["D%d%d" % (par, h)], tt(out, pt, sh, A.subtract))
+            else:
+                S(H, ["pT%d" % h], ["sg%d" % h], act(sh, pt, F.Sign, bias=-0.0625, scale=-1.0))
+                PE(2 * H, ["Ib", "cg%d" % h, "D%d%d" % (par, h)], ["pT%d" % h],
+                   mms([(pt, B("Ib"), out, True, False), (pt, B("Ib"), B("cg", H * h, H * h + H), False, False)]))
+                PE(H, ["Ib", "sg%d" % h], ["pT%d" % h], mms([(pt, B("Ib"), sh, False, True)]))
+                S(H, ["pT%d" % h], ["D%d%d" % (par, h)], act(out, pt, F.Copy))
+        V(56, ["pS"], ["wr"], ts(B("wr"), B("pS", 0, 56), float(RING - 128 * (t + 1)), float(RING), A.is_ge, A.mult))
+        V(56, ["pS", "wr"], ["P"], tt(B("P"), B("pS", 0, 56), B("wr"), A.subtract))
+        if t + 1 < STEPS:
+            lists(t + 1)
+
+    def send(kind, key, rd, arr, nbytes, ways=None):
+        op("pool", nbytes, rd, [], None, send=(kind, key), arr=arr, ways=ways or {s: "D" for s in arr.values()})
+
+    def crazor(m):
+        o = 12 * m
+        PE(1024, ["W8", "D10", "D11"], ["pR"],
+           mms([(B("pR", 0, 56), B("W8", 15 - j, 143 - j), B("D", 1 + 2 * j, L, 32), j == 0, j == 15) for j in range(16)]))
+        V(56, ["pR", "thc"], ["cut"], ts(B("cut"), B("pR", 0, 56), B("thc", m, m + 1), None, A.is_ge))
+        PE(128, ["cut", "Bm", "Um"], ["pR"], mms([(B("pR", 64, 120), B("Bm"), B("cut"), True, True),
+                                                  (B("pR", 128, 184), B("Um"), B("cut"), True, True)]))
+        V(56, ["pR", "ones"], ["Tc"], lambda g, T: g.vector.tensor_tensor_scan(T.Tc[:], T.ones[:], T.pR[:, 64:120], 0.0, A.mult, A.add))
+        V(56, ["pR", "Tc"], ["cum"], tt(B("cum"), B("pR", 128, 184), B("Tc"), A.add))
+        for j in range(6):
+            S(80, ["Tc", "kcol"], ["acc%d" % j],
+              lambda g, T, j=j: g.scalar.activation(T.junk[:, 56 * j:56 * j + 55], T.Tc[:, 0:55], F.Sign, bias=T.kcol[:, j:j + 1],
+                                                    scale=-1.0, accum_out=T.acc[:, j:j + 1]))
+        ac = ["acc%d" % j for j in range(6)]
+        V(6, ac, ["colk"], ts(B("colk"), B("acc"), 0.5, 27.5, A.mult, A.add))
+        V(96, ["cum", "colk", "xr"], ["fl"], tt(B("fl"), G("cum", 56, "colk", 0, 6), B("xr", 0, 96), A.is_le), "t")
+        V(6, ac, ["col32"], ts(B("col32"), B("acc"), 16.0, 880.0, A.mult, A.add))
+        PE(256, ["col32", "Wi"], ["pR"], mms([(B("pR", 192, 198), B("Wi", 0, 128), B("col32"), True, False)]))
+        PE(1024, ["W2", "fl"], ["pR"],
+           mms([(B("pR", 192, 198), B("W2", 15 - j, 143 - j), B("fl", j, 96, 16), False, j == 15) for j in range(16)]))
+        for j in range(2):
+            V(6, ["pR"], ["src%d_%d" % (m, j)], ts(B("srcl", o + 6 * j, o + 6 * j + 6), B("pR", 192, 198), float(j), None, A.add))
+        sl = ["src%d_0" % m, "src%d_1" % m]
+        S(192, DA + ["Dd"] + sl, ["pc%d" % m], act(B("pc", PC * m, PC * m + 192), G("D", XW, "srcl", o, o + 12), F.Copy), GK)
+        V(12, sl, ["pg%d" % m], ts(B("pc", PC * m + 192, PC * m + 204), B("srcl", o, o + 12), float(L), 4096.0, A.is_ge, A.mult))
+        send("c", m, ["pc%d" % m, "pg%d" % m], {"lc%d" % m: "rc%d" % m}, 256 * PW)
+        V(12, sl, ["o12"], cp(B("o12"), B("srcl", o, o + 12)))
+        V(12, ["o12", "pg%d" % m], ["o12"], tt(B("o12"), B("o12"), B("pc", PC * m + 192, PC * m + 204), A.max))
+        V(12, ["o12", "lc%d" % m], ["y12"], tt(B("y12"), B("o12"), B("lc", PC * m + 192, PC * m + 204), A.max))
+        V(12, ["y12", "dump0", "dump1"], ["y12"], tt(B("y12"), B("y12"), B("dump"), A.min))
+        V(12, ["y12"], ["dst%d" % m], cp(B("dstl", o, o + 12), B("y12")))
+        V(192, ["dst%d" % m, "lc%d" % m], DA + ["Dd"], cp(G("D", XW, "dstl", o, o + 12), B("lc", PC * m, PC * m + 192)), "s")
+
+    def xtake(m, j, n):
+        o, b = 12 * m + 6 * j, 192 * m + 96 * j
+        x = "eo"[j]
+        S(96 * n, XA + ["Xd", "src%d_0" % m, "src%d_1" % m], ["px%s%d" % (x, m)],
+          act(B("px", b, b + 96 * n), G("X", XW, "srcl", o, o + 6 * n), F.Copy), GK)
+        send("x", (b, 96 * n, "r%s%d" % (x, m)), ["px%s%d" % (x, m)], {"lx%s%d" % (x, m): "r%s%d" % (x, m)}, 512 * 96 * n)
+
+    def xput(m, j, n):
+        o, b = 12 * m + 6 * j, 192 * m + 96 * j
+        V(96 * n, ["dst%d" % m, "lx%s%d" % ("eo"[j], m)], XA + ["Xd"], cp(G("X", XW, "dstl", o, o + 6 * n), B("lx", b, b + 96 * n)), "s")
+        if j == 0:
+            V(1, ["X00"], ["Xm"], cp(B("X", L, L + 1), B("X", 0, 1)))
+
+    def xstep(t):
+        par = t % 2
+        o = 56 * t
+        win, wt = ("rawx", ["rawx", "rawm"]) if t == 0 else ("X", XA)
+        razor = par == 1 and t < STEPS - 1
+        if razor and XEARLY:
+            xtake(t // 2, 0, 1)
+
+        def zmm(h, st):
+            c0, c1, _e, _eo, pa, ao = CH[h]
+            r = 16 * (t % 8)
+            ps = [p for p in pieces(t - 1) if p[0] == h]
+            alone = ADD[par][h] == "v"
+            if st and not alone:
+                ps = [(h, [p[4] for p in ps], 16 * c0, 16 * (c1 - c0))]
+            for p in ps:
+                z0, a0 = K * (t - 1) + p[2], ao + p[2] - 16 * c0
+                rd = p[1] if len(p) == 4 else [p[4]]
+                if t - 1 in CODE:
+                    V(p[3], rd, ["u" + rd[0]], ts(B("zl", z0, z0 + p[3]), B("z16", z0, z0 + p[3]), 1.0 / CODE[t - 1], None, A.mult))
+                    rd = ["u" + rd[0]]
+                PE(4 * p[3], ["Wz"] + rd, [pa],
+                   mms([(B(pa, a0, a0 + p[3]), B("Wz", r, r + 128), B("zl", z0, z0 + p[3]), st, alone or (not st and p is ps[-1]))]))
+
+        for h, (c0, c1, e, eo, pa, ao) in enumerate(CH):
+            n, j0 = 16 * (c1 - c0), 16 * c0
+            s0, ah, dh, eh = K * t + j0, B("a", j0, j0 + n), B("d", j0, j0 + n), B(e, eo, eo + n)
+            PE(512, ["E8", "phi%d_0" % t, "phi%d_1" % t], [e],
+               mms([(B(e, eo + j, eo + n, 8), B("E8", 128 * j, 128 * j + 128), B("phi", 112 * t + 2 * c0, 112 * t + 2 * c1), True, True) for j in range(8)]))
+            if t and not ZLAST[par][h]:
+                zmm(h, True)
+            S(n, wt + ["offv%d" % t], ["a%d" % h], act(ah, G(win, L, "offv", o + c0, o + c1), F.Copy), "g")
+            V(n, wt + ["offw%d" % t, "a%d" % h], ["d%d" % h], tt(dh, G(win, L + 1, "offw", o + c0, o + c1), ah, A.subtract), "t")
+            if h in LATE.get(t, ()):
+                V(n, ["d%d" % h, e], ["d%d" % h], tt(dh, dh, eh, A.mult))
+                if t + 1 < STEPS:
+                    V(n, ["a%d" % h, "d%d" % h], ["s%d_%d" % (t, h)], tt(B("s", s0, s0 + n), ah, dh, A.add), 2.0)
+            else:
+                V(n, ["d%d" % h, e], [e], tt(eh, dh, eh, A.mult))
+                V(n, ["a%d" % h, e], ["s%d_%d" % (t, h)], tt(B("s", s0, s0 + n), ah, eh, A.add))
+            for x in ops[-4:]:
+                x["lead"] = -LEAD * h
+            if t + 1 < STEPS:
+                ps = [p for p in pieces(t) if p[0] == h]
+                rd = "s%d_%d" % (t, h)
+                if t in CODE:
+                    V(n, [rd], ["c" + rd], ts(B("s16", s0, s0 + n), B("s", s0, s0 + n), CODE[t], None, A.mult))
+                    rd = "c" + rd
+                send("z", (t, h), [rd], {p[4]: p[4] for p in ps}, (256 if t in CODE else 512) * ps[0][3], {p[4]: p[1] for p in ps})
+        for h, (c0, c1, e, eo, pa, ao) in enumerate(CH):
+            n, j0 = 16 * (c1 - c0), 16 * c0
+            s0, out = K * t + j0, B("X", par + 2 * j0, 2 * (j0 + n), 2)
+            if t == 0:
+                S(n, ["s0_%d" % h], ["X0%d" % h], act(out, B("s", s0, s0 + n), F.Tanh, scale=0.625))
+                if h == 0:
+                    S(1, ["s0_0"], ["Xm"], act(B("X", L, L + 1), B("s", 0, 1), F.Tanh, scale=0.625))
+                continue
+            ph = B(pa, ao, ao + n)
+            if h in LATE.get(t, ()):
+                zl = ZLAST[par][h]
+                PE(4 * n, ["Wi", "a%d" % h], [pa], mms([(ph, B("Wi", 0, 128), B("a", j0, j0 + n), zl, False)]))
+                PE(4 * n, ["Wi", "d%d" % h], [pa], mms([(ph, B("Wi", 0, 128), B("d", j0, j0 + n), False, not zl)]))
+                if zl:
+                    zmm(h, False)
+            elif ADD[par][h] == "v":
+                if ZLAST[par][h]:
+                    zmm(h, True)
+                V(n, ["s%d_%d" % (t, h), pa], [pa], tt(ph, B("s", s0, s0 + n), ph, A.add))
+            else:
+                PE(4 * n, ["Wi", "s%d_%d" % (t, h)], [pa], mms([(ph, B("Wi", 0, 128), B("s", s0, s0 + n), ZLAST[par][h], not ZLAST[par][h])]))
+                if ZLAST[par][h]:
+                    zmm(h, False)
+            S(n, [pa], ["X%d%d" % (par, h)], act(out, ph, F.Tanh, scale=0.625))
+            if par == 0 and h == 0:
+                S(1, [pa], ["Xm"], act(B("X", L, L + 1), B(pa, ao, ao + 1), F.Tanh, scale=0.625))
+            if t == STEPS - 1:
+                dma("sync", "st", 1024 * (j0 + n), ["X0%d" % h, "X1%d" % h], [],
+                    lambda g, T, j0=j0, n=n: g.sync.dma_start(T.yx[:, 2 * j0:2 * (j0 + n)], T.X[:, 2 * j0:2 * (j0 + n)]))
+        if razor:
+            m = t // 2
+            if XEARLY:
+                xtake(m, 1, 1)
+                xput(m, 0, 1)
+                xput(m, 1, 1)
+            else:
+                xtake(m, 0, 2)
+                xput(m, 0, 2)
+
+    lists(0)
+    for t in range(STEPS):
+        part[:] = ["c%d" % (t % 2), 0]
+        cstep(t)
+        if t % 2 == 1 and t < STEPS - 1:
+            crazor(t // 2)
+    part[:] = ["e", 0]
+    PE(16 * 112, ["W8"] + DA, ["pR"],
+       mms([(B("pR", 0, 112), B("W8", 15 - j, 143 - j), B("D", 112 * j, 112 * j + 112), j == 0, j == 15) for j in range(16)]))
+    V(112, ["pR"], ["ycf"], ts(B("ycf"), B("pR", 0, 112), 128.0, None, A.add))
+    dma("sync", "st", 0, ["ycf"], [], lambda g, T: g.sync.dma_start(T.yc[:], T.ycf[:]))
+    V(56, ["P"], ["Pi"], ts(B("Pi"), B("P"), 128.0 * STEPS, None, A.add))
+    V(56, ["Pi"], ["yp0"], ts(B("ypi", 0, 56), B("Pi"), 8, None, A.arith_shift_right))
+    V(56, ["Pi"], ["yp1"], ts(B("ypi", 56, 112), B("Pi"), 255, None, A.bitwise_and))
+    V(112, ["yp0", "yp1"], ["ypf"], cp(B("ypf"), B("ypi")))
+    dma("sync", "st", 0, ["ypf"], [], lambda g, T: g.sync.dma_start(T.yp[:], T.ypf[:]))
+    for t in range(STEPS):
+        part[:] = ["x%s" % (t % 2 if 0 < t < STEPS - 1 else "ab"[t % 2]), 0]
+        xstep(t)
+    return ops
+
+
+def order(ops):
+    lastw, readers, arrival = {}, {}, {}
+    for i, o in enumerate(ops):
+        dep, arr = set(), []
+        for k in o["rd"]:
+            if k in arrival:
+                arr.append(arrival[k])
+            elif k in lastw:
+                dep.add(lastw[k])
+            if k in BANKS:
+                dep.update(j for j in readers.get(k, []) if ops[j]["q"] != o["q"])
+        for k in o["wr"]:
+            if k in lastw:
+                dep.add(lastw[k])
+            dep.update(readers.get(k, []))
+        dep.discard(i)
+        for k in o["rd"]:
+            readers.setdefault(k, []).append(i)
+        for k in o["wr"]:
+            lastw[k] = i
+            readers[k] = []
+        for k, sem in o.get("arr", {}).items():
+            arrival[k] = (i, sem)
+        o["dep"], o["wait_arr"] = sorted(dep), arr
+    return rank_calls(ops)
+
+
+def rank_calls(ops):
+    n = len(ops)
+    pre = [set(o["dep"]) | set(j for j, _s in o["wait_arr"]) for o in ops]
+    suc = [[] for _ in ops]
+    for i in range(n):
+        for j in pre[i]:
+            suc[j].append(i)
+    prio = [0.0] * n
+    M = MODEL
+    for i in range(n - 1, -1, -1):
+        ops[i]["dur"], ops[i]["lat"] = cost(ops[i], M)
+        far = max(land(ops[i], 0.0, M, {}).values()) if "send" in ops[i] else 0.0
+        prio[i] = ops[i]["dur"] + ops[i]["lat"] + far + max([prio[j] + M["sem"] for j in suc[i]], default=0.0)
+    for i in range(n):
+        a, b = ops[i]["cls"]
+        prio[i] += (AHEAD if a[0] in "ci" else 0.0) + (0.5 * (ord(SHIFT[a][b]) - 77) if b < len(SHIFT.get(a, "")) else 0.0) + ops[i].get("lead", 0.0) + (1000.0 * (100 - i) if ops[i]["q"] in ("sync", "pool") and not pre[i] else 0.0)
+    left = [len(p) for p in pre]
+    ready = {i: 0.0 for i in range(n) if not left[i]}
+    free, seq, end, landed, busy = {}, [], 0.0, {}, {}
+    while ready:
+        st = {i: max(r, free.get(ops[i]["q"], 0.0)) for i, r in ready.items()}
+        b = min(st, key=lambda i: (st[i], -prio[i]))
+        c = max((i for i in st if ops[i]["q"] == ops[b]["q"] and st[i] <= st[b] + SLACK), key=lambda i: prio[i])
+        o = ops[c]
+        o["start"] = st[c]
+        free[o["q"]] = st[c] + o["dur"]
+        o["done"] = st[c] + o["dur"] + o["lat"]
+        if "send" in o:
+            landed.update(land(o, o["done"], M, busy))
+        end = max(end, o["done"])
+        seq.append(c)
+        del ready[c]
+        for j in suc[c]:
+            left[j] -= 1
+            if not left[j]:
+                ready[j] = max([ops[k]["done"] + (0.0 if ops[k]["q"] == ops[j]["q"] == "pe" else M["sem"]) for k in ops[j]["dep"]]
+                               + [landed[s] + M["sem"] for _k, s in ops[j]["wait_arr"]])
+    return seq, end
+
+
+def polish(ops, seq, rounds):
+    n = len(ops)
+    qs = [o["q"] for o in ops]
+    ms = [dict(MODEL, **x) for x in SPREAD]
+    co = [[cost(o, M) for o in ops] for M in ms]
+    dep = [[(j, qs[j] == o["q"] == "pe") for j in o["dep"]] for o in ops]
+    pre = [set(o["dep"]) | set(j for j, _s in o["wait_arr"]) for o in ops]
+    arr = [o["wait_arr"] for o in ops]
+    snd = ["send" in o for o in ops]
+
+    def run(sq, m, p0, old):
+        M, c, sm = ms[m], co[m], ms[m]["sem"]
+        done, rel, why, landed, snap = (list(old[0]), list(old[1]), list(old[2]), dict(old[3]), dict(old[4])) if old else ([0.0] * n, [0.0] * n, [0] * n, {}, {})
+        last, busy = {}, {}
+        for i in sq[:p0]:
+            last[qs[i]] = i
+            if snd[i]:
+                busy = snap[i]
+        busy = dict(busy)
+        for i in sq[p0:]:
+            w = last.get(qs[i], -1)
+            s = rel[w] if w >= 0 else 0.0
+            w = -2 - w
+            for j, p in dep[i]:
+                x = done[j] if p else done[j] + sm
+                if x > s:
+                    s, w = x, j
+            for j, a in arr[i]:
+                if landed[a] + sm > s:
+                    s, w = landed[a] + sm, j
+            rel[i] = s = s + c[i][0]
+            done[i] = s + c[i][1]
+            why[i] = w
+            last[qs[i]] = i
+            if snd[i]:
+                landed.update(land(ops[i], s, M, busy))
+                snap[i] = dict(busy)
+        return done, rel, why, landed, snap, max(done)
+
+    rng = np.random.default_rng(7)
+    st = [run(seq, m, 0, None) for m in range(len(ms))]
+    cur = best = sum(x[5] for x in st)
+    keep = seq
+    for r in range(rounds):
+        s = st[r % len(ms)]
+        i, arcs = s[0].index(s[5]), []
+        while s[2][i] != -1:
+            w = s[2][i]
+            if w < -1:
+                w = -2 - w
+                if w not in pre[i] and qs[i] != "sync":
+                    arcs.append((w, i))
+            i = w
+        u, v = arcs[int(rng.integers(len(arcs)))]
+        pu, pv = seq.index(u), seq.index(v)
+        need, needq, want = [v], set(), set(pre[v])
+        for x in reversed(seq[pu + 1:pv]):
+            if x in want or qs[x] in needq:
+                need.append(x)
+                needq.add(qs[x])
+                want |= pre[x]
+        if u in want:
+            continue
+        ns = set(need)
+        sq = seq[:pu] + need[::-1] + [x for x in seq[pu:pv] if x not in ns] + seq[pv + 1:]
+        new = [run(sq, m, pu, st[m]) for m in range(len(ms))]
+        val = sum(x[5] for x in new)
+        if val < cur + HEAT * (1.0 - r / rounds) * float(rng.exponential()):
+            seq, st, cur = sq, new, val
+            if val < best:
+                best, keep = val, sq
+    done = run(keep, 0, 0, None)[0]
+    for i in range(n):
+        ops[i]["done"] = done[i]
+    return keep
+
+
+def helpers(T, topo):
+    place = lambda c: (topo.host(c), topo.chip(c))
+    busy = set(place(c) for c in T.cores)
+    used, out = set(), {}
+    names = sorted(set(w for v in ROUTE.values() for ws in v for w in ws if w != "D"))
+    n = len(T.cores)
+    for w in names:
+        for r, c in enumerate(T.cores):
+            d = T.cores[(r + 1) % n]
+            if w[0] == "A":
+                cand = [x for x in topo.cores_of(c) if topo.die(x) != topo.die(c) and topo.may_write(x, d)]
+                out[r, w] = cand[int(w[1:]) % len(cand)]
+            else:
+                cand = [x for x in range(WORLD) if place(x) not in busy and topo.same_plane(c, x) and topo.die(x) == topo.die(c)
+                        and topo.may_write(x, d) and place(x) not in used]
+                cand.sort(key=lambda x: topo.host(x) != topo.host(c))
+                out[r, w] = cand[0]
+                used.add(place(cand[0]))
+    return out
+
+
+def bits(es):
+    return sum(1 << e for e in es)
+
+
+PLAN = {}
+
+
+def rank_program(g, core, T, topo):
+    rank = T.rank_of(core)
+    n = len(T.cores)
+    if "seq" not in PLAN:
+        PLAN["ops"] = build()
+        PLAN["seq"], PLAN["end"] = order(PLAN["ops"])
+        PLAN["seq"] = polish(PLAN["ops"], PLAN["seq"], ROUNDS)
+        PLAN["help"] = helpers(T, topo)
+    ops, hp = PLAN["ops"], PLAN["help"]
+    if rank is None:
+        sent = 0
+        for (r, w), c in hp.items():
+            if c != core:
+                continue
+            d = T.cores[(r + 1) % n]
+            rid, pid = topo.addr(d, core)
+            ne = len(topo.engines(core, d))
+            for t in range(STEPS - 1):
+                for p in pieces(t):
+                    if p[1] == w:
+                        ap = T["z16" if t in CODE else "zl"][:, K * t + p[2]:K * t + p[2] + p[3]]
+                        g.wait_ge(T.sem[p[4]], first_hop(T, topo, hp, r, t, p))
+                        g.remote_dma(ap, ap, T.sem[p[4]], T.sem.sent, pid, rid, topo.mask(core, d))
+                        sent += ne
+        if sent:
+            g.wait_ge(T.sem.sent, sent)
+        return
+    nxt, prv = T.cores[(rank + 1) % n], (rank - 1) % n
+    Q = {"pool": g, "pe": g.tensor, "dve": g.vector, "act": g.scalar, "sync": g.sync}
+    known = {q: {} for q in Q}
+    count, clock, sent = {}, {}, [0]
+    far = topo.engines(core, nxt)
+
+    def arrives(sem):
+        for t in range(STEPS - 1):
+            for p in pieces(t):
+                if p[4] == sem:
+                    if p[1] == "D":
+                        return first_hop(T, topo, hp, prv, t, p)
+                    return len(topo.engines(hp[prv, p[1]], core))
+        return len(topo.engines(T.cores[prv], core))
+
+    def wait(q, sem, val, more):
+        if known[q].get(sem, 0) < val:
+            Q[q].wait_ge(T.sem[sem], val)
+            known[q][sem] = val
+            for k, v in more.items():
+                known[q][k] = max(known[q].get(k, 0), v)
+
+    def remote(kind, key):
+        rid, pid = topo.addr(nxt, core)
+        if kind == "c":
+            g.remote_dma(T.lc[:, PC * key:PC * key + PW], T.pc[:, PC * key:PC * key + PW], T.sem["rc%d" % key], T.sem.sent, pid, rid, bits(far))
+            sent[0] += len(far)
+        elif kind == "x":
+            b, w, sem = key
+            g.remote_dma(T.lx[:, b:b + w], T.px[:, b:b + w], T.sem[sem], T.sem.sent, pid, rid, bits(far))
+            sent[0] += len(far)
+        else:
+            t, h = key
+            trs = []
+            for p in pieces(t):
+                if p[0] == h:
+                    d = nxt if p[1] == "D" else hp[rank, p[1]]
+                    r2, p2 = topo.addr(d, core)
+                    es = hop_engines(T, topo, hp, rank, t, p)
+                    a = K * t + p[2]
+                    trs.append(RemoteDMATransfer(dst_ids=[DstId(rid=r2, pnc=p2)], dma_engine_mask=bits(es), remote_sem=T.sem[p[4]],
+                                                 src=T["s16" if t in CODE else "s"][:, a:a + p[3]],
+                                                 dst=T["z16" if t in CODE else "zl"][:, a:a + p[3]]))
+                    sent[0] += len(es)
+            g.remote_dma_fused(trs, local_sem=T.sem.sent)
+
+    for i in PLAN["seq"]:
+        o = ops[i]
+        q = o["q"]
+        need = [j for j in o["dep"] if not (q == "pe" and ops[j]["q"] == "pe")]
+        for j in sorted(need, key=lambda j: -ops[j]["done"]):
+            sem, val, more = clock[j]
+            wait(q, sem, val, more)
+        for _j, sem in o["wait_arr"]:
+            wait(q, sem, arrives(sem), {})
+        if "send" in o:
+            remote(*o["send"])
+            continue
+        sem, inc = o.get("sem", q), o.get("inc", 1)
+        o["fn"](g, T).then_inc(T.sem[sem], inc)
+        count[sem] = count.get(sem, 0) + inc
+        clock[i] = (sem, count[sem], dict(known[q]))
+    for sem, val in count.items():
+        wait("pool", sem, val, {})
+    g.wait_ge(T.sem.sent, sent[0])
+
+
+def hop_engines(T, topo, hp, r, t, p):
+    c = T.cores[r]
+    far = topo.engines(c, T.cores[(r + 1) % len(T.cores)])
+    mine = [x for x in pieces(t) if x[0] == p[0] and (x[1][0] == "A") == (p[1][0] == "A")]
+    pool = far if p[1][0] != "A" else [e for e in topo.engines(c, hp[r, p[1]]) if e not in far]
+    k = len(pool) // len(mine)
+    i = mine.index(p)
+    return pool[i * k:(i + 1) * k]
+
+
+def first_hop(T, topo, hp, r, t, p):
+    return len(hop_engines(T, topo, hp, r, t, p))

@@ -1,116 +1,109 @@
-import numpy as np
 from concourse.bass import DstId, RemoteDMATransfer
 from concourse.mybir import AluOpType, ActivationFunctionType
 
 A = AluOpType
 F = ActivationFunctionType
-L, K, H, STEPS, NR, CAP, WORLD = 1792, 896, 448, 10, 4, 96, 256
-XW = L + 2 + 2 * CAP
-RING = 16 * L
+L, K, H, STEPS, NR, WORLD = 1792, 896, 448, 10, 4, 256
+LC = 62
+SRC = 32 * LC
+GATE = 2048
+XW = SRC + GATE
 PW, PC = 204, 208
 
-CH = [(0, 28, "pE0", 0, "pA0", 0), (28, 56, "pE1", 0, "pA1", 0)]
-ROUTE = {0: [["A0", "B0"], ["D"]], 1: [["A0", "B0"], ["A1", "B1"]]}
-ZLAST = {0: [False] * 4, 1: [True] * 4}
-XEARLY = True
-CG0, CG = "av", {0: "aa", 1: "aa"}
-DN = {0: "vv", 1: "vv"}
-ADD = {0: "pv", 1: "pv"}
-LATE = {}
-CODE = {}
-SLACK, LEAD, AHEAD = 0.15, 1.0, 2.0
-SHIFT = {'c0': 'QMMMKNOLQKMMMJQIJHIN', 'c1': 'MMMMMMMQRMMMQOMMMRMMMJMPHIMKNLMMMMMMMMTLQMJMNPQ', 'e': 'MSMMIMOP',
-         'i': 'MONMOKMPMKMTOMMMMQMMMMMMMINUMMPPMMMLNMMNMQMQILMNM', 'x0': 'MMMPMKMOKOMOMQMMKKMM', 'x1': 'IQMMLGMOMMLNNLJMIIMKMMOIMM',
-         'xa': 'QHNMLNQMMRRLMMM', 'xb': 'MMKMMMMMMMMLMMMMKIM'}
-MODEL = dict(cy=0.001, py=0.0005, fix=0.06, g=1.55, t=1.8, s=3.5, sem=0.1, issue=0.6, up=2.0, link=60e3, chip=120e3, eng=15e3, hbm=200e3)
-SPREAD = [{}, dict(py=0.00075, g=1.2, t=1.2, s=2.0, sem=0.15, issue=0.9, up=2.6, link=45e3, eng=11e3),
-          dict(cy=0.00115, py=0.00058, g=1.9, t=2.0, s=5.0, sem=0.07, issue=0.4, up=1.5, link=100e3, eng=20e3)]
-ROUNDS, HEAT = 8000, 0.3
+FIRST = [(0, 28, 0, "s", ["A0", "B0"]), (28, 56, 1, "s", ["D"])]
+EVEN = [(0, 28, 0, "p", ["A0", "B0"]), (28, 56, 1, "v", ["D"])]
+ODD = [(0, 28, 0, "w", ["A0", "A1"]), (28, 56, 1, "v", ["D"])]
+EIGHTH = [(0, 14, 0, "p", ["A0", "B0"]), (28, 42, 1, "u", ["D"]), (14, 28, 0, "p", ["D"]), (42, 56, 1, "u", ["D"])]
+LAST = [(0, 14, 0, "w", []), (28, 42, 1, "w", []), (14, 28, 0, "w", []), (42, 56, 1, "w", [])]
+CH = [FIRST, ODD] + [EVEN, ODD] * 3 + [EIGHTH, LAST]
+ZLAST = {0: False, 1: True}
+CG = ["av", "aa"] * 5
+
+ORDER = {
+    "pe": """e.pR<D00@1 CO.pS<Iw@1 CE.pS<P e.pR<D10@1 XE.pE0<E XE.pE1<E CE.pT0<D00 ce.pT1<D01 ce.pT0<D00 ce.pT1<cg1 ce.pT0<cg0
+        ce.pS<P ce.pS<cg0 co.pR<D10 ce0.pS<P co.pT1<D11 CE.pT1<D01 CE.pT1<cg1 ce0.pT0<rawc ce0.pT1<rawc ce0.pT0<cg0 ce0.pT1<cg1
+        ce0.pS<cg0 i.pR<sel xe.pE1<E xe.pE0<E co.pT0<D10 xe.pA1<z_2 xe.pA0<z_0 co.pT1<cg1 co.pT0<cg0 CE.pS<cg0 XE.pA0<z_0
+        XE.pA0<s_0 CE.pT0<cg0 xe.pA0<s_0 co.pR<cg0 co0.pT0<D10 xe0.pE1<E co0.pT1<D11 xe0.pE0<E co0.pR<D10 co0.pT1<cg1 co0.pS<P
+        co0.pT0<cg0 co.pR<sg0 co0.pR<cg0 co0.pR<sg0 co0.pS<cg0 xo.pE0<E r.pR<Bm xo.pE1<E co.pS<P CO.pS<P XE.pA0<z_1 XE.pA0<s_2
+        XO.pE0<E XO.pE1<E CO.pT0<D10 XO.pA1<a_1 XO.pA1<z_2 XO.pA0<a_0 CO.pT1<D11 XO.pA0<z_0 CO.pT0<cg0 XO.pA0<z_1 XO.pA1<a_3
+        XO.pA1<z_4 CO.pT1<cg1 XO.pA0<a_2 XO.pA0<z_3 CO.pS<cg0 co.pS<cg0 xo.pA0<a_0 xo0.pA0<a_0 xo0.pE0<E r.pR<acc1 r.pR<fl
+        xo.pA0<z_0 xo0.pE1<E co0.pS<Iw xo0.pA1<z_2 xo0.pA0<z_0 xo.pA0<z_1 xo.pA1<z_2 co.pS<Iw xo0.pA0<z_1""",
+    "dve": """xo.s_1@1 xo.arg0@1 xo.arg2@1 co.offv@1 r.dst@1 co.vf@1 xo0.arg0@1 r.D00@1 co0.vf@1 XO.pA1'@1 XO.s_2@1 CO.D11@1 XO.pA0'@1
+        CO.D10@1 e.Pi@1 i.ci2 i.ci3 i.ci4 i.ci1 i.cf i.Wi i.cf5 i.kcol i.Wh i.cf8 i.cf6 i.P i.offv co.phi@1 ce.cg1 co0.phi@1
+        xo0.X00@1 i.E0 i.cf7 i.keep i.E3 i.vf xo.X00@1 i.phi i.E1 i.E2 i.sel ce0.cg1 i.thb i.D10 i.offw e.yp1@1 e.yp0@1 ce.D01
+        co.offw@1 CE.cg1 e.ypf@1 e.ycf@1 ce.D00 XE.d2 XE.d0 XE.pE1 XE.pE0 XE.s_1 XE.d1 XE.s_0 XE.d3 XE.pE0' ce.offv ce.vf
+        co0.offw@1 ce.phi i.Bm i.rawm ce0.D00 ce0.offv i.thc ce0.D01 xe0.d0 ce0.vf xe0.pE0 xe0.d2 xe0.s_0 xe0.pE1 xe.d0 xe.d2
+        xe.pE0 xe.s_0 xe.pE1 xe.s_1 xe0.s_1 ce0.phi CE.offv XE.pA1 XE.s_2 CE.vf XE.pE1' CE.phi XE.s_3 XE.pA1' CE.D00 CE.offw
+        CE.D01 xe.pA1 ce.offw co.D10 co.D11 XO.d3 XO.d2 XO.d1 XO.s_1 XO.d0 XO.pA1 XO.s_0 XO.pA0 co0.D11 ce0.offw r.cum co0.D10
+        xo.d0 xo0.d0 r.colk r.fl xo0.s_0 xo.s_0 xo.d2 xo0.d2 r.src_0 xo.pE1 XO.s_3 xo0.pE1 xo0.s_1 co0.offv r.y xo0.arg2""",
+    "act": """xo0.pxe@1 CO.sg1@1 XO.X13@1 CO.sg0@1 CO.P@1 CO.wr@1 XO.X11@1 xo0.X12@1 xo0.pxo@1 xo.pxo@1 xo.X10@1 xo.X12@1 i.Dd i.c8
+        i.argd i.Wz i.I8 i.kcol i.Wn i.cut i.Ib ce0.cg0 xo0.X10@1 ce.cg0 co0.phm_0@1 co.phm_1@1 co.phm_0@1 co0.phm_1@1 ce.sg1
+        xo.Xm@1 xo0.Xm@1 ce.sg0 xo.X00@1 xo0.X00@1 ce.P XE.a_1 XE.a_0 CE.cg0 XE.a_2 XE.pA1 XE.a_3 xe.a_0 xe.a_1 ce.Dd co.cg1
+        co.cg0 CE.P CE.sg1 i.phm_1 i.phm_0 i.W2 ce0.sg0 ce0.sg1 ce0.P xe0.a_0 ce0.Dd xe0.a_1 co0.cg1 co0.cg0 co0.sg1 co0.sg0
+        xe0.X00 i.Iw ce.phm_1 co.sg1 co.sg0 ce.phm_0 xe.X00 XE.X00 CE.sg0 XE.X02 XE.pA1' XE.Xm XE.X01 CE.phm_1 XE.X03 CE.phm_0
+        xe.Xm xe.X02 xe0.Xm r.cut xe0.X02 ce0.phm_1 xo0.a_0 xo.a_0 XO.a_3 XO.a_1 XO.a_2 XO.a_0 CE.Dd CO.cg0 XO.X12 CO.cg1 XO.X10
+        ce0.phm_0 r.acc3 r.acc4 r.acc2 r.acc5 r.acc1 r.acc0 r.pg xo0.a_1 co0.wr co0.P xo.a_1 co.P co.wr r.own0 r.own1 r.pc
+        xo.pxe""",
+    "pool": """r.sendcpc@1 xo.sendxpxe@1 i.xr i.ci0 i.xe i.Xd xo0.sendxpxe@1 xo.sendxpxo@1 xo0.sendzs_1@1 xo0.sendxpxo@1 xo.sendzs_1@1
+        i.arg0 i.X10 i.Lm i.Um xe.sendzs_0 XE.sendzs_0 XE.sendzs_1 xe0.sendzs_0 xe.sendzs_1 XE.sendzs_3 XE.sendzs_2 xe0.sendzs_1
+        r.sendcpg xo.sendzs_0 xo0.sendzs_0""",
+    "sync": """XO.stX02@1 XO.stX00@1 i.posi i.rawc i.thi i.rawx XO.stX03@1 XO.stX01@1 e.stypf@1 e.stycf@1""",
+}
 
 SCRATCH = {
     "rawx": ("sbuf", [128, L + 16], "bfloat16"), "rawc": ("sbuf", [128, L], "bfloat16"),
-    "X": ("sbuf", [128, XW + 6], "float32"), "D": ("sbuf", [128, XW + 6], "bfloat16"),
-    "posi": ("sbuf", [128, 56], "int32"), "P": ("sbuf", [128, 56], "float32"), "wr": ("sbuf", [128, 56], "float32"),
-    "Pi": ("sbuf", [128, 56], "int32"), "fr": ("sbuf", [128, 56], "int32"),
-    "offv": ("sbuf", [128, 560], "uint16"), "offw": ("sbuf", [128, 560], "uint16"), "phi": ("sbuf", [128, 1120], "bfloat16"),
+    "X": ("sbuf", [128, XW], "float32"), "D": ("sbuf", [128, XW], "bfloat16"), "arg": ("sbuf", [128, SRC], "float32"),
+    "posi": ("sbuf", [128, 56], "int32"), "P": ("sbuf", [128, 56], "float32"), "wr": ("sbuf", [128, 56], "bfloat16"),
+    "Pi": ("sbuf", [128, 56], "int32"), "vf": ("sbuf", [128, 56], "float32"),
+    "offv": ("sbuf", [128, 560], "uint16"), "offw": ("sbuf", [128, 560], "uint16"),
+    "phi": ("sbuf", [128, 560], "bfloat16"), "phm": ("sbuf", [128, 1120], "bfloat16"),
     "cg": ("sbuf", [128, K], "bfloat16"), "sg": ("sbuf", [128, K], "bfloat16"),
-    "a": ("sbuf", [128, K], "float32"), "d": ("sbuf", [128, K], "float32"),
+    "a": ("sbuf", [128, K * STEPS], "float32"), "d": ("sbuf", [128, K], "float32"),
     "s": ("sbuf", [128, K * STEPS], "float32"), "zl": ("sbuf", [128, K * (STEPS - 1)], "float32"),
-    "s16": ("sbuf", [128, K * (STEPS - 1)], "uint16"), "z16": ("sbuf", [128, K * (STEPS - 1)], "uint16"),
     "pc": ("sbuf", [128, PC * NR], "bfloat16"), "lc": ("sbuf", [128, PC * NR], "bfloat16"),
     "px": ("sbuf", [128, 192 * NR], "float32"), "lx": ("sbuf", [128, 192 * NR], "float32"),
     "srcl": ("sbuf", [128, 12 * NR], "uint16"), "dstl": ("sbuf", [128, 12 * NR], "uint16"),
-    "cut": ("sbuf", [128, 56], "bfloat16"), "Tc": ("sbuf", [128, 56], "float32"), "cum": ("sbuf", [128, 56], "float32"),
-    "junk": ("sbuf", [128, 336], "bfloat16"), "acc": ("sbuf", [128, 6], "float32"), "colk": ("sbuf", [128, 6], "uint16"),
-    "col32": ("sbuf", [128, 6], "float32"), "fl": ("sbuf", [128, 96], "bfloat16"),
-    "o12": ("sbuf", [128, 12], "float32"), "y12": ("sbuf", [128, 12], "float32"),
+    "cut": ("sbuf", [128, LC + 2], "bfloat16"), "cum": ("sbuf", [128, 128], "float32"),
+    "junk": ("sbuf", [128, 6 * 64], "bfloat16"), "acc": ("sbuf", [128, 6], "float32"), "colk": ("sbuf", [128, 6], "uint16"),
+    "fl": ("sbuf", [128, 96], "bfloat16"), "own": ("sbuf", [128, 12], "float32"), "y12": ("sbuf", [128, 12], "float32"),
     "thi": ("sbuf", [128, 4], "int32"), "thb": ("sbuf", [128, 4], "bfloat16"), "thc": ("sbuf", [128, 4], "float32"),
     "ci": ("sbuf", [128, 8], "int32"), "cf": ("sbuf", [128, 12], "float32"),
     "xr": ("sbuf", [128, 256], "float32"), "xe": ("sbuf", [128, 256], "bfloat16"),
-    "Wi": ("sbuf", [128, 256], "float32"), "Wz": ("sbuf", [128, 256], "float32"),
-    "Ib": ("sbuf", [128, 128], "bfloat16"), "W8": ("sbuf", [128, 144], "bfloat16"), "W2": ("sbuf", [128, 144], "bfloat16"),
-    "E8": ("sbuf", [128, 1024], "bfloat16"), "Bm": ("sbuf", [128, 128], "bfloat16"), "Um": ("sbuf", [128, 128], "bfloat16"),
-    "sel": ("sbuf", [128, 128], "bfloat16"), "ones": ("sbuf", [128, 56], "float32"),
-    "kcol": ("sbuf", [128, 6], "float32"), "dump": ("sbuf", [128, 12], "float32"),
+    "Wi": ("sbuf", [128, 256], "float32"), "Wz": ("sbuf", [128, 256], "float32"), "Ib": ("sbuf", [128, 128], "bfloat16"),
+    "Wh": ("sbuf", [128, 144], "bfloat16"), "W2": ("sbuf", [128, 144], "bfloat16"), "Wn": ("sbuf", [128, 144], "bfloat16"),
+    "E": ("sbuf", [128, 1024], "bfloat16"),
+    "Bm": ("sbuf", [128, 128], "bfloat16"), "Lm": ("sbuf", [128, 128], "bfloat16"), "Um": ("sbuf", [128, 128], "bfloat16"),
+    "sel": ("sbuf", [128, 128], "bfloat16"), "keep": ("sbuf", [128, 128], "float32"), "c8": ("sbuf", [128, 128], "bfloat16"),
+    "Iw": ("sbuf", [128, 128], "bfloat16"), "I8": ("sbuf", [128, 128], "bfloat16"),
+    "kcol": ("sbuf", [128, 12], "float32"),
     "ypi": ("sbuf", [128, 112], "int32"), "ypf": ("sbuf", [128, 112], "float32"), "ycf": ("sbuf", [128, 112], "float32"),
     "pE0": ("psum", [128, 512], "float32"), "pE1": ("psum", [128, 512], "float32"),
     "pA0": ("psum", [128, 512], "float32"), "pA1": ("psum", [128, 512], "float32"),
     "pT0": ("psum", [128, 512], "float32"), "pT1": ("psum", [128, 512], "float32"),
     "pS": ("psum", [128, 512], "float32"), "pR": ("psum", [128, 512], "float32"),
 }
+BANKS = ("pE0", "pE1", "pA0", "pA1", "pT0", "pT1", "pS", "pR")
 
 
 def pieces(t):
     out = []
-    for h, c in enumerate(CH):
-        ways = ROUTE[t % 2][h]
-        n = 16 * (c[1] - c[0]) // len(ways)
-        for i, w in enumerate(ways):
+    for h, c in enumerate(CH[t]):
+        n = 16 * (c[1] - c[0]) // len(c[4])
+        for i, w in enumerate(c[4]):
             out.append((h, w, 16 * c[0] + i * n, n, "z%d_%d" % (t, len(out))))
     return out
 
 
-def land(o, at, M, busy):
-    out = {}
-    for sem, w in o["ways"].items():
-        like = sum((x[0] == "A") == (w[0] == "A") for x in o["ways"].values())
-        rate, t = M["eng"] * 8 / like, at + M["up"]
-        if w != "D":
-            t += o["n"] / min(rate, M["chip"]) + M["issue"] + M["up"]
-            rate = M["eng"] * 8
-        k = w[0] if w[0] == "A" else w
-        busy[k] = max(t, busy.get(k, 0.0)) + o["n"] / M["link"]
-        out[sem] = max(busy[k], t + o["n"] / rate)
-    return out
-
-
-def cost(o, M):
-    q, n = o["q"], o["n"]
-    if "send" in o:
-        return M["issue"], 0.0
-    if q == "sync":
-        return 0.1, 2.0 + n / M["hbm"]
-    if q == "pool":
-        return 0.13 + 2 * n * M["cy"], 0.0
-    if q == "pe":
-        return M["fix"] + n * M["py"], 0.0
-    return M["fix"] + max(64, n * M.get(o["k"], o["k"])) * M["cy"], 0.0
-
-
-SEMAPHORES = (["pe", "dve", "act", "pool", "sent", "l0", "l1", "l2", "l3", "l4", "st"]
+SEMAPHORES = (["pe", "dve", "act", "pool", "sent", "l0", "l1", "l2", "l3", "st"]
               + [p[4] for t in range(STEPS - 1) for p in pieces(t)]
-              + ["r%s%d" % (x, m) for x in ("c", "e", "o") for m in range(NR)])
-BANKS = ("pE0", "pE1", "pA0", "pA1", "pT0", "pT1", "pS", "pR")
+              + ["r%s%d" % (x, m) for x in ("c", "g", "e", "o") for m in range(NR)])
 
 
 def build():
-    ops, part = [], ["i", 0]
+    ops, part = [], ["i"]
 
     def op(q, n, rd, wr, fn, k=1.0, **kw):
-        o = dict(q=q, n=n, k=k, rd=list(rd), wr=list(wr), fn=fn, cls=(part[0], part[1]))
-        part[1] += 1
-        o.update(kw)
-        ops.append(o)
+        ops.append(dict(q=q, n=n, k=k, rd=list(rd), wr=list(wr), fn=fn, cls=(part[0], len(ops)), **kw))
 
     def V(n, rd, wr, fn, k=1.0):
         op("dve", n, rd, wr, fn, k)
@@ -121,11 +114,13 @@ def build():
     def PE(cyc, rd, wr, fn):
         op("pe", cyc, rd, wr, fn)
 
+    def val(x, T):
+        return x if isinstance(x, (int, float)) else x(T)
+
     def ts(o, i, s1, s2, o0, o1=None):
         if o1 is None:
-            return lambda g, T: g.vector.tensor_scalar(o(T), i(T), s1(T) if s1 is not None and not isinstance(s1, (int, float)) else s1, None, o0)
-        return lambda g, T: g.vector.tensor_scalar(o(T), i(T), s1(T) if not isinstance(s1, (int, float)) else s1,
-                                                   s2(T) if not isinstance(s2, (int, float)) else s2, o0, o1)
+            return lambda g, T: g.vector.tensor_scalar(o(T), i(T), val(s1, T), None, o0)
+        return lambda g, T: g.vector.tensor_scalar(o(T), i(T), val(s1, T), val(s2, T), o0, o1)
 
     def tt(o, i0, i1, alu):
         return lambda g, T: g.vector.tensor_tensor(o(T), i0(T), i1(T), alu)
@@ -134,7 +129,7 @@ def build():
         return lambda g, T: g.vector.tensor_copy(o(T), i(T))
 
     def act(o, i, f, **kw):
-        return lambda g, T: g.scalar.activation(o(T), i(T), f, **kw)
+        return lambda g, T: g.scalar.activation(o(T), i(T), f, **{k: val(x, T) for k, x in kw.items()})
 
     def B(name, a=None, b=None, c=None):
         return lambda T: T[name][:, a:b:c] if c else T[name][:, a:b]
@@ -150,264 +145,281 @@ def build():
             return r
         return fn
 
+    def tracks(out, w, rhs, first, last):
+        return mms([(out, B(w, 15 - j, 143 - j), rhs(j), first and j == 0, last and j == 15) for j in range(16)])
+
     def col(j):
         return B("cf", j, j + 1)
 
-    def dma(q, sem, nbytes, rd, wr, fn):
-        op(q, nbytes, rd, wr, fn, sem=sem, inc=16)
+    def dma(sem, nbytes, rd, wr, fn):
+        op("sync", nbytes, rd, wr, fn, sem=sem, inc=16)
 
-    XA = ["X%d%d" % (p, h) for p in range(2) for h in range(len(CH))] + ["Xm"]
+    def iota(o, pat):
+        return lambda g, T: g.iota(o(T), pat, 0, 0, allow_small_or_imprecise_dtypes=True)
+
+    def select(o, i, pat, cmp, cm):
+        return lambda g, T: g.affine_select(o(T), i(T), pat, cmp, 0.0, 0, cm)
+
+    def send(kind, key, rd, arr, nbytes, ways=None, fold=1):
+        op("pool", nbytes, rd, [], None, send=(kind, key), arr=arr, ways=ways or {s: "D" for s in arr.values()}, fold=fold)
+
+    def quarters(name, c0, c1):
+        return ["%s%d" % (name, q) for q in range(c0 // 14, (c1 + 13) // 14)]
+
+    def over(t):
+        return 16 * (t % 2)
+
+    def kept(t):
+        return t < STEPS - 2 and all(c[3] in "vw" for c in CH[t])
+
+    XA = quarters("X0", 0, 56) + quarters("X1", 0, 56) + ["Xm"]
+    AA = quarters("arg0", 0, 56) + quarters("arg1", 0, 56) + ["argd"]
     DA = ["D00", "D01", "D10", "D11"]
-    GK = "g"
+    ET = ["E%d" % j for j in range(4)]
 
-    dma("sync", "l0", 0, [], ["posi"], lambda g, T: g.sync.dma_start(T.posi[:], T.pos[:]))
-    dma("sync", "l1", 460e3, [], ["rawc"], lambda g, T: g.sync.dma_start(T.rawc[:], T.ctl[:]))
-    dma("sync", "l2", 920e3, [], ["rawx"], lambda g, T: g.sync.dma_start(T.rawx[:, 0:L], T.tape[:]))
-    dma("sync", "l3", 920e3, [], ["thi"], lambda g, T: g.sync.dma_start(T.thi[0:8, :], T.th[:]))
+    dma("l0", 0, [], ["posi"], lambda g, T: g.sync.dma_start(T.posi[:], T.pos[:]))
+    dma("l1", 460e3, [], ["rawc"], lambda g, T: g.sync.dma_start(T.rawc[:], T.ctl[:]))
+    dma("l2", 460e3, [], ["rawx"], lambda g, T: g.sync.dma_start(T.rawx[:, 0:L], T.tape[:]))
+    dma("l3", 0, [], ["thi"], lambda g, T: g.sync.dma_start(T.thi[0:8, :], T.th[:]))
 
     op("pool", 1, [], ["ci0"], lambda g, T: g.iota(T.ci[:, 0:1], [[0, 1]], 0, 1))
-    op("pool", 256, [], ["xr"], lambda g, T: g.iota(T.xr[:], [[0, 2], [1, 128]], 0, 0, allow_small_or_imprecise_dtypes=True))
-    op("pool", 256, [], ["xe"], lambda g, T: g.iota(T.xe[:], [[1, 2], [16, 8], [0, 16]], 0, 0, allow_small_or_imprecise_dtypes=True))
+    op("pool", 256, [], ["xr"], iota(B("xr"), [[0, 2], [1, 128]]))
+    op("pool", 256, [], ["xe"], iota(B("xe"), [[1, 2], [16, 8], [0, 16]]))
     for j, msk in enumerate((112, 15, 119, 8)):
         V(1, ["ci0"], ["ci%d" % (j + 1)], ts(B("ci", j + 1, j + 2), B("ci", 0, 1), msk, None, A.bitwise_and))
     V(5, ["ci%d" % j for j in range(5)], ["cf"], cp(B("cf", 0, 5), B("ci", 0, 5)))
     V(1, ["cf"], ["cf5"], ts(col(5), col(1), 15.0, None, A.add))
-    V(1, ["cf"], ["cf6"], ts(col(6), col(4), 0.0, 0.0625, A.is_equal, A.mult))
-    V(1, ["cf"], ["cf7"], ts(col(7), col(4), 8.0, 0.0625, A.is_equal, A.mult))
     V(1, ["cf"], ["cf8"], ts(col(8), col(0), 16.0, None, A.mult))
     V(256, ["cf", "xr"], ["Wi"], ts(B("Wi"), B("xr"), col(0), None, A.is_equal))
     S(256, ["Wi"], ["Wz"], act(B("Wz"), B("Wi"), F.Copy, scale=0.6))
     S(128, ["Wi"], ["Ib"], act(B("Ib"), B("Wi", 0, 128), F.Copy))
-    V(144, ["cf5", "xr"], ["W8"], ts(B("W8"), B("xr", 0, 144), col(5), 8.0, A.is_equal, A.mult))
-    S(144, ["W8"], ["W2"], act(B("W2"), B("W8"), F.Copy, scale=0.25))
+    S(128, ["Wi"], ["Iw"], act(B("Iw"), B("Wi", 0, 128), F.Copy, scale=-L / 2))
+    V(144, ["cf5", "xr"], ["Wh"], ts(B("Wh"), B("xr", 0, 144), col(5), 0.5, A.is_equal, A.mult))
+    S(144, ["Wh"], ["W2"], act(B("W2"), B("Wh"), F.Copy, scale=0.25))
+    S(144, ["Wh"], ["Wn"], act(B("Wn"), B("Wh"), F.Copy, scale=-1.0))
+    V(1, ["cf"], ["cf6"], ts(col(6), col(4), 0.0, None, A.is_equal))
+    V(1, ["cf"], ["cf7"], ts(col(7), col(4), 8.0, None, A.is_equal))
     for j in range(4):
-        V(256, ["cf", "xe"] + ["E8"] * (j == 3), ["E8"] if j == 3 else ["E8_%d" % j],
-          ts(B("E8", 256 * j, 256 * j + 256), B("xe"), 2.0 * j, col(3), A.add, A.is_equal), 0.5)
-    ops[-1]["rd"] = ["cf", "xe", "E8_0", "E8_1", "E8_2"]
-    V(128, ["cf", "xe"], ["Bm"], ts(B("Bm"), B("xe", 0, 128), col(1), None, A.is_equal), 0.5)
-    V(128, ["cf", "xr"], ["Um"], ts(B("Um"), B("xr", 0, 128), col(0), -1.0, A.is_lt, A.mult))
-    V(128, ["Um", "Bm"], ["Um"], tt(B("Um"), B("Um"), B("Bm"), A.mult))
+        V(256, ["cf", "xe"], [ET[j]], ts(B("E", 256 * j, 256 * j + 256), B("xe"), 2.0 * j, col(3), A.add, A.is_equal), 0.5)
+    V(128, ["cf", "xe"], ["Bm"], ts(B("Bm"), B("xe", 0, 128), col(1), 0.5, A.is_equal, A.mult), 0.5)
+    op("pool", 128, ["Bm"], ["Lm"], select(B("Lm"), B("Bm"), [[1, 128]], A.is_ge, -1))
+    op("pool", 128, ["Bm"], ["Um"], select(B("Um"), B("Bm"), [[-1, 128]], A.is_gt, 1))
     V(128, ["cf8", "xe"], ["sel"], ts(B("sel"), B("xe", 0, 128), col(8), None, A.is_equal), 0.5)
-    V(6, ["cf", "xr"], ["kcol"], ts(B("kcol"), B("xr", 0, 96, 16), col(2), 0.5, A.add, A.add))
-    for j in range(2):
-        V(6, ["kcol"], ["dump%d" % j], ts(B("dump", 6 * j, 6 * j + 6), B("kcol"), 2.0, float(L + 1 + j), A.mult, A.add))
-    V(56, [], ["ones"], lambda g, T: g.vector.memset(T.ones[:], 1.0))
-    V(100, [], ["Dd"], lambda g, T: g.vector.memset(T.D[:, L:XW], 0.0))
-    S(1500, ["xr"], ["Xd", "Xm"], act(B("X", L, XW), B("xr", 0, XW - L), F.Tanh))
+    V(6, ["cf", "xr"], ["kcol"], ts(B("kcol", 0, 6), B("xr", 0, 96, 16), col(2), 0.5, A.add, A.add))
+    S(6, ["kcol"], ["kcol2"], act(B("kcol", 6, 12), B("kcol", 0, 6), F.Copy))
+    V(124, ["xr"], ["keep"], ts(B("keep", 0, 2 * LC), B("xr", 0, 2 * LC), float(LC), None, A.not_equal))
+    S(LC + 1, ["xr"], ["cut"], act(B("cut", 0, LC + 1), B("xr", 0, LC + 1), F.Sign, bias=-0.5))
+    S(124, ["xr"], ["c8"], act(B("c8", 0, 2 * LC), B("xr", 0, 2 * LC), F.Copy, scale=0.0, bias=8.0))
+    S(192, ["xr"], ["Dd"], act(B("D", L, SRC), B("xr", 0, SRC - L), F.Copy, scale=0.0))
+    S(1500, ["xr"], ["argd"], act(B("arg", L, SRC), B("xr", 0, SRC - L), F.Tanh))
+    op("pool", L, [], quarters("arg1", 0, 56) + quarters("arg0", 0, 56), iota(B("arg", 0, L), [[0, L]]))
+    op("pool", SRC - L, [], ["Xd", "Xm"], iota(B("X", L, SRC), [[0, SRC - L]]))
     V(4, ["thi"], ["thb"], lambda g, T: g.vector.tensor_copy(T.thb[0:8, :], T.thi[0:8, :]))
     PE(64, ["thb", "sel"], ["pR"], lambda g, T: g.tensor.matmul(T.pR[:, 0:4], T.sel[0:8, :], T.thb[0:8, :], True, True))
-    V(4, ["pR"], ["thc"], ts(B("thc"), B("pR", 0, 4), -128.0, None, A.add))
+    V(4, ["pR"], ["thc"], ts(B("thc"), B("pR", 0, 4), -1.0, 128.5, A.mult, A.add))
     V(1, ["rawx"], ["rawm"], cp(B("rawx", L, L + 1), B("rawx", 0, 1)))
-    for p in range(2):
-        V(K, ["rawc"], ["D%d0" % p, "D%d1" % p], ts(B("D", p, L, 2), B("rawc", p, L, 2), 0.125, -1.0, A.mult, A.add), 0.5)
-    for h, c in enumerate(CH):
-        S(16 * (c[1] - c[0]), ["rawx"], ["X1%d" % h], act(B("X", 1 + 32 * c[0], 32 * c[1], 2), B("rawx", 1 + 32 * c[0], 32 * c[1], 2), F.Copy))
-    V(56, ["posi"], ["P"], cp(B("P"), B("posi")))
+    V(K, ["rawc"], ["D10", "D11"], ts(B("D", 1, L, 2), B("rawc", 1, L, 2), 0.125, -1.0, A.mult, A.add), 0.5)
+    S(128, ["Wi"], ["I8"], act(B("I8"), B("Wi", 0, 128), F.Copy, scale=0.125))
+    op("pool", K, ["rawx"], quarters("X1", 0, 56), select(B("X", 1, L, 2), B("rawx", 1, L, 2), [[0, K]], A.is_ge, 0))
+    V(56, ["posi"], ["P"], ts(B("P"), B("posi"), 0.0625, -0.46875, A.mult, A.add))
+
+    wrapped = (B("pS", 64, 120), "pS")
+
+    def drift(t):
+        return 8.0 * (t + (t > 0)) - L / 2 * (t // 2)
 
     def lists(t):
-        src, tok = (B("posi"), "posi") if t == 0 else (B("P"), "P")
-        V(56, [tok], ["offv%d" % t], ts(B("offv", 56 * t, 56 * t + 56), src, 0.0625, 8.0 * t - 0.46875, A.mult, A.add))
-        V(56, [tok], ["offw%d" % t], ts(B("offw", 56 * t, 56 * t + 56), src, 0.0625, 8.0 * t + 0.53125, A.mult, A.add))
-        if t:
-            V(56, ["P"], ["Pi"], ts(B("Pi"), B("P"), 128.0 * t, None, A.add))
-        V(56, ["Pi" if t else "posi"], ["fr"], ts(B("fr"), B("Pi") if t else B("posi"), 15, None, A.bitwise_and))
+        o = 56 * t
+        src, tok = (B("pS", 0, 56), "pS") if t % 2 else wrapped if t else (B("P"), "P")
+        V(56, [tok], ["offv%d" % t], ts(B("offv", o, o + 56), src, drift(t), None, A.add))
+        V(56, ["offv%d" % t], ["offw%d" % t], ts(B("offw", o, o + 56), B("offv", o, o + 56), 1.0, None, A.add))
+        V(56, ["offv%d" % t], ["vf"], ts(B("vf"), B("offv", o, o + 56), -drift(t) - 0.46875, None, A.add))
+        if t % 2:
+            src, tok = B("P"), "P"
+        V(56, ["vf", tok], ["phi%d" % t], tt(B("phi", o, o + 56), src, B("vf"), A.subtract))
         for j in range(2):
-            V(56, ["fr", "cf%d" % (6 + j)], ["phi%d_%d" % (t, j)], ts(B("phi", 112 * t + j, 112 * t + 112, 2), B("fr"), col(6 + j), None, A.mult))
+            S(56, ["phi%d" % t, "cf%d" % (6 + j)], ["phm%d_%d" % (t, j)],
+              act(B("phm", 2 * o + j, 2 * o + 112, 2), B("phi", o, o + 56), F.Copy, scale=col(6 + j)))
 
     def cstep(t):
-        par = t % 2
-        o = 56 * t
-        PE(256, ["P", "Wi"], ["pS"], mms([(B("pS", 0, 56), B("Wi", 0, 128), B("P"), True, False)]))
+        par, o = t % 2, 56 * t
+        razor = par and t < STEPS - 1
+        back = [(B("pS", 0, 56), B("Iw"), B("wr"), False, False)] * (t > 0 and not par)
+        PE(256 + 64 * len(back), ["Wi", "P"] + ["Iw", "wr"] * len(back), ["pS"], mms([(B("pS", 0, 56), B("Wi", 0, 128), B("P"), True, False)] + back))
         for h in range(2):
-            PE(H, ["Ib", "D%d%d" % (par, h)], ["pT%d" % h],
-               mms([(B("pT%d" % h, 0, H), B("Ib"), B("D", par + K * h, K * (h + 1), 2), True, False)]))
+            w, old, tok = ("Ib", "D", "D%d%d" % (par, h)) if t else ("I8", "rawc", "rawc")
+            PE(H, [w, tok], ["pT%d" % h], mms([(B("pT%d" % h, 0, H), B(w), B(old, par + K * h, K * (h + 1), 2), True, False)]))
         for h in range(2):
-            out, w = B("cg", H * h, H * h + H), G("D" if t else "rawc", L, "offv", o + 28 * h, o + 28 * h + 28)
-            rd = (DA if t else ["rawc"]) + ["offv%d" % t]
-            if (CG0 if t == 0 else CG[par])[h] == "a":
-                S(H, rd, ["cg%d" % h], act(out, w, F.Copy) if t else act(out, w, F.Copy, scale=0.125, bias=-1.0), "g")
+            out, w = B("cg", H * h, H * h + H), G("D" if t else "rawc", L + over(t), "offv", o + 28 * h, o + 28 * h + 28)
+            rd = (DA if t else ["rawc"]) + ["offv%d" % t] + ["Dd"] * par
+            if CG[t][h] == "a":
+                S(H, rd, ["cg%d" % h], act(out, w, F.Copy) if t else act(out, w, F.Copy, scale=0.125, bias=-2.0), "g")
             else:
-                V(H, rd, ["cg%d" % h], cp(out, w) if t else ts(out, w, 0.125, -1.0, A.mult, A.add), "g")
+                V(H, rd, ["cg%d" % h], cp(out, w) if t else ts(out, w, 0.125, -2.0, A.mult, A.add), "g")
         for h in range(2):
             PE(H, ["Ib", "cg%d" % h], ["pT%d" % h], mms([(B("pT%d" % h, 0, H), B("Ib"), B("cg", H * h, H * h + H), False, True)]))
-        PE(1024, ["W8", "cg0", "cg1"], ["pS"],
-           mms([(B("pS", 0, 56), B("W8", 15 - m, 143 - m), B("cg", m, K, 16), False, m == 15) for m in range(16)]))
+        PE(1024, ["Wh", "cg0", "cg1"], ["pS"], tracks(B("pS", 0, 56), "Wh", lambda j: B("cg", j, K, 16), False, True))
+        if razor:
+            PE(1024, ["Wh", "D10", "D11"], ["pR"], tracks(B("pR", 0, 56), "Wh", lambda j: B("D", 1 + 2 * j, L, 32), True, False))
+            PE(1024, ["Wh", "cg0", "cg1"], ["pR"], tracks(B("pR", 0, 56), "Wh", lambda j: B("cg", j, K, 16), False, False))
         for h in range(2):
             pt, sh, out = B("pT%d" % h, 0, H), B("sg", H * h, H * h + H), B("D", par + K * h, K * (h + 1), 2)
-            if DN[par][h] == "v":
-                S(H, ["pT%d" % h], ["sg%d" % h], act(sh, pt, F.Sign, bias=0.0625))
-                V(H, ["pT%d" % h, "sg%d" % h], ["D%d%d" % (par, h)], tt(out, pt, sh, A.subtract))
-            else:
-                S(H, ["pT%d" % h], ["sg%d" % h], act(sh, pt, F.Sign, bias=-0.0625, scale=-1.0))
-                PE(2 * H, ["Ib", "cg%d" % h, "D%d%d" % (par, h)], ["pT%d" % h],
-                   mms([(pt, B("Ib"), out, True, False), (pt, B("Ib"), B("cg", H * h, H * h + H), False, False)]))
-                PE(H, ["Ib", "sg%d" % h], ["pT%d" % h], mms([(pt, B("Ib"), sh, False, True)]))
-                S(H, ["pT%d" % h], ["D%d%d" % (par, h)], act(out, pt, F.Copy))
-        V(56, ["pS"], ["wr"], ts(B("wr"), B("pS", 0, 56), float(RING - 128 * (t + 1)), float(RING), A.is_ge, A.mult))
-        V(56, ["pS", "wr"], ["P"], tt(B("P"), B("pS", 0, 56), B("wr"), A.subtract))
+            S(H, ["pT%d" % h], ["sg%d" % h], act(sh, pt, F.Sign, bias=0.0625))
+            V(H, ["pT%d" % h, "sg%d" % h], ["D%d%d" % (par, h)], tt(out, pt, sh, A.subtract))
+        if razor:
+            PE(1024, ["Wn", "sg0", "sg1"], ["pR"], tracks(B("pR", 0, 56), "Wn", lambda j: B("sg", j, K, 16), False, True))
+        if par:
+            S(56, ["pS"], ["wr"], act(B("wr"), B("pS", 0, 56), F.Sign, bias=drift(t) + 8.5 - L))
+            S(56, ["pS"], ["P"], act(B("P"), B("pS", 0, 56), F.Copy))
+            PE(320, ["Wi", "Iw", "wr", "P"], ["pS"], mms([(wrapped[0], B("Wi", 0, 128), B("P"), True, False), (wrapped[0], B("Iw"), B("wr"), False, True)]))
+        else:
+            S(56, ["pS"], ["P"], act(B("P"), B("pS", 0, 56), F.Copy))
+            S(16, ["D00", "D10"], ["Dd"], act(B("D", L, L + 16), B("D", 0, 16), F.Copy))
         if t + 1 < STEPS:
             lists(t + 1)
 
-    def send(kind, key, rd, arr, nbytes, ways=None):
-        op("pool", nbytes, rd, [], None, send=(kind, key), arr=arr, ways=ways or {s: "D" for s in arr.values()})
-
     def crazor(m):
-        o = 12 * m
-        PE(1024, ["W8", "D10", "D11"], ["pR"],
-           mms([(B("pR", 0, 56), B("W8", 15 - j, 143 - j), B("D", 1 + 2 * j, L, 32), j == 0, j == 15) for j in range(16)]))
-        V(56, ["pR", "thc"], ["cut"], ts(B("cut"), B("pR", 0, 56), B("thc", m, m + 1), None, A.is_ge))
-        PE(128, ["cut", "Bm", "Um"], ["pR"], mms([(B("pR", 64, 120), B("Bm"), B("cut"), True, True),
-                                                  (B("pR", 128, 184), B("Um"), B("cut"), True, True)]))
-        V(56, ["pR", "ones"], ["Tc"], lambda g, T: g.vector.tensor_tensor_scan(T.Tc[:], T.ones[:], T.pR[:, 64:120], 0.0, A.mult, A.add))
-        V(56, ["pR", "Tc"], ["cum"], tt(B("cum"), B("pR", 128, 184), B("Tc"), A.add))
+        o, b = 12 * m, PC * m
+        tot, dl = B("pR", 64, 64 + LC), B("pR", 64 + LC, 64 + 2 * LC)
+        now, bef = B("cut", 1, LC + 1), B("cut", 0, LC)
+        S(56, ["pR", "thc"], ["cut"], act(B("cut", 1, 57), B("pR", 0, 56), F.Sign, bias=B("thc", m, m + 1), scale=16.0))
+        PE(320, ["cut", "Bm", "Lm", "Um", "c8", "Ib"], ["pR"],
+           mms([(B("pR", 64, 64 + 2 * LC), B("Ib"), B("c8", 0, 2 * LC), True, False), (tot, B("Bm"), now, False, False),
+                (dl, B("Lm"), now, False, False), (dl, B("Um"), bef, False, True)]))
+        V(2 * LC, ["pR", "keep"], ["cum"], lambda g, T: g.vector.tensor_tensor_scan(
+            T.cum[:, 2:2 + 2 * LC], T.keep[:, 0:2 * LC], T.pR[:, 64:64 + 2 * LC], 0.0, A.mult, A.add))
         for j in range(6):
-            S(80, ["Tc", "kcol"], ["acc%d" % j],
-              lambda g, T, j=j: g.scalar.activation(T.junk[:, 56 * j:56 * j + 55], T.Tc[:, 0:55], F.Sign, bias=T.kcol[:, j:j + 1],
-                                                    scale=-1.0, accum_out=T.acc[:, j:j + 1]))
+            S(85, ["cum", "kcol"], ["acc%d" % j], act(B("junk", 64 * j, 64 * j + LC - 1), B("cum", 2, LC + 1), F.Sign, bias=B("kcol", j, j + 1),
+                                                      scale=-1.0, accum_out=B("acc", j, j + 1)))
         ac = ["acc%d" % j for j in range(6)]
-        V(6, ac, ["colk"], ts(B("colk"), B("acc"), 0.5, 27.5, A.mult, A.add))
-        V(96, ["cum", "colk", "xr"], ["fl"], tt(B("fl"), G("cum", 56, "colk", 0, 6), B("xr", 0, 96), A.is_le), "t")
-        V(6, ac, ["col32"], ts(B("col32"), B("acc"), 16.0, 880.0, A.mult, A.add))
-        PE(256, ["col32", "Wi"], ["pR"], mms([(B("pR", 192, 198), B("Wi", 0, 128), B("col32"), True, False)]))
-        PE(1024, ["W2", "fl"], ["pR"],
-           mms([(B("pR", 192, 198), B("W2", 15 - j, 143 - j), B("fl", j, 96, 16), False, j == 15) for j in range(16)]))
+        V(6, ac, ["colk"], ts(B("colk"), B("acc"), 0.5, (LC - 1) / 2, A.mult, A.add))
+        V(96, ["cum", "colk", "xr"], ["fl"],
+          tt(B("fl"), lambda T: T.cum[:, 64:64 + LC].indirect(T.colk[:, 0:6]), B("xr", 0, 96), A.is_le), "t")
+        R = B("pR", 192, 198)
+        PE(256, ac + ["Wi"], ["pR"], mms([(R, B("Wi", 0, 128), B("acc"), True, False)]))
+        PE(1024, ["W2", "fl"], ["pR"], tracks(R, "W2", lambda j: B("fl", j, 96, 16), False, True))
+        u = GATE / 2
         for j in range(2):
-            V(6, ["pR"], ["src%d_%d" % (m, j)], ts(B("srcl", o + 6 * j, o + 6 * j + 6), B("pR", 192, 198), float(j), None, A.add))
-        sl = ["src%d_0" % m, "src%d_1" % m]
-        S(192, DA + ["Dd"] + sl, ["pc%d" % m], act(B("pc", PC * m, PC * m + 192), G("D", XW, "srcl", o, o + 12), F.Copy), GK)
-        V(12, sl, ["pg%d" % m], ts(B("pc", PC * m + 192, PC * m + 204), B("srcl", o, o + 12), float(L), 4096.0, A.is_ge, A.mult))
-        send("c", m, ["pc%d" % m, "pg%d" % m], {"lc%d" % m: "rc%d" % m}, 256 * PW)
-        V(12, sl, ["o12"], cp(B("o12"), B("srcl", o, o + 12)))
-        V(12, ["o12", "pg%d" % m], ["o12"], tt(B("o12"), B("o12"), B("pc", PC * m + 192, PC * m + 204), A.max))
-        V(12, ["o12", "lc%d" % m], ["y12"], tt(B("y12"), B("o12"), B("lc", PC * m + 192, PC * m + 204), A.max))
-        V(12, ["y12", "dump0", "dump1"], ["y12"], tt(B("y12"), B("y12"), B("dump"), A.min))
-        V(12, ["y12"], ["dst%d" % m], cp(B("dstl", o, o + 12), B("y12")))
-        V(192, ["dst%d" % m, "lc%d" % m], DA + ["Dd"], cp(G("D", XW, "dstl", o, o + 12), B("lc", PC * m, PC * m + 192)), "s")
+            S(6, ["pR"], ["own%d" % j], act(B("own", 6 * j, 6 * j + 6), R, F.Copy, scale=16.0 / u, bias=(16.0 * (LC - 1) + j) / u + 1.0))
+        V(12, ["own0", "own1"], ["src%d_0" % m, "src%d_1" % m], ts(B("srcl", o, o + 12), B("own"), u, -u, A.mult, A.add))
+        S(192, DA + ["Dd", "src%d_0" % m, "src%d_1" % m], ["pc%d" % m], act(B("pc", b, b + 192), G("D", SRC, "srcl", o, o + 12), F.Copy), "g")
+        S(12, ["cum", "kcol", "kcol2"], ["pg%d" % m], act(B("pc", b + 192, b + PW), B("kcol"), F.Sign, bias=B("cum", 57, 58), scale=-1.0))
+        send("c", (b + 192, 12, "rg%d" % m), ["pg%d" % m], {"lg%d" % m: "rg%d" % m}, 256 * 12)
+        send("c", (b, 192, "rc%d" % m), ["pc%d" % m], {"lc%d" % m: "rc%d" % m}, 256 * 192)
+        V(12, ["own0", "own1", "lg%d" % m], ["y12"], tt(B("y12"), B("own"), B("lc", b + 192, b + PW), A.subtract))
+        V(12, ["y12"], ["dst%d" % m], ts(B("dstl", o, o + 12), B("y12"), u, None, A.mult))
+        V(192, ["dst%d" % m, "lc%d" % m], DA + ["Dd"], cp(G("D", XW, "dstl", o, o + 12), B("lc", b, b + 192)), "s")
 
-    def xtake(m, j, n):
-        o, b = 12 * m + 6 * j, 192 * m + 96 * j
-        x = "eo"[j]
-        S(96 * n, XA + ["Xd", "src%d_0" % m, "src%d_1" % m], ["px%s%d" % (x, m)],
-          act(B("px", b, b + 96 * n), G("X", XW, "srcl", o, o + 6 * n), F.Copy), GK)
-        send("x", (b, 96 * n, "r%s%d" % (x, m)), ["px%s%d" % (x, m)], {"lx%s%d" % (x, m): "r%s%d" % (x, m)}, 512 * 96 * n)
+    def xtake(m, j):
+        o, b, x = 12 * m + 6 * j, 192 * m + 96 * j, "eo"[j]
+        if kept(2 * m + j):
+            S(96, AA + ["src%d_%d" % (m, j)], ["px%s%d" % (x, m)], act(B("px", b, b + 96), G("arg", SRC, "srcl", o, o + 6), F.Copy, scale=0.625), "g")
+        else:
+            S(96, XA + ["Xd", "src%d_%d" % (m, j)], ["px%s%d" % (x, m)], act(B("px", b, b + 96), G("X", SRC, "srcl", o, o + 6), F.Copy), "g")
+        send("x", (b, 96, "r%s%d" % (x, m)), ["px%s%d" % (x, m)], {"lx%s%d" % (x, m): "r%s%d" % (x, m)}, 512 * 96)
 
-    def xput(m, j, n):
+    def xput(m, j):
         o, b = 12 * m + 6 * j, 192 * m + 96 * j
-        V(96 * n, ["dst%d" % m, "lx%s%d" % ("eo"[j], m)], XA + ["Xd"], cp(G("X", XW, "dstl", o, o + 6 * n), B("lx", b, b + 96 * n)), "s")
+        rd, out = ["dst%d" % m, "lx%s%d" % ("eo"[j], m)], G("X", XW, "dstl", o, o + 6)
+        if kept(2 * m + j):
+            S(96, rd, XA + ["Xd"], act(out, B("lx", b, b + 96), F.Tanh), "s")
+        else:
+            V(96, rd, XA + ["Xd"], cp(out, B("lx", b, b + 96)), "s")
         if j == 0:
-            V(1, ["X00"], ["Xm"], cp(B("X", L, L + 1), B("X", 0, 1)))
+            S(1, ["X00"], ["Xm"], act(B("X", L, L + 1), B("X", 0, 1), F.Copy))
 
     def xstep(t):
-        par = t % 2
-        o = 56 * t
+        par, o = t % 2, 56 * t
         win, wt = ("rawx", ["rawx", "rawm"]) if t == 0 else ("X", XA)
-        razor = par == 1 and t < STEPS - 1
-        if razor and XEARLY:
-            xtake(t // 2, 0, 1)
-
-        def zmm(h, st):
-            c0, c1, _e, _eo, pa, ao = CH[h]
-            r = 16 * (t % 8)
-            ps = [p for p in pieces(t - 1) if p[0] == h]
-            alone = ADD[par][h] == "v"
-            if st and not alone:
-                ps = [(h, [p[4] for p in ps], 16 * c0, 16 * (c1 - c0))]
-            for p in ps:
-                z0, a0 = K * (t - 1) + p[2], ao + p[2] - 16 * c0
-                rd = p[1] if len(p) == 4 else [p[4]]
-                if t - 1 in CODE:
-                    V(p[3], rd, ["u" + rd[0]], ts(B("zl", z0, z0 + p[3]), B("z16", z0, z0 + p[3]), 1.0 / CODE[t - 1], None, A.mult))
-                    rd = ["u" + rd[0]]
-                PE(4 * p[3], ["Wz"] + rd, [pa],
-                   mms([(B(pa, a0, a0 + p[3]), B("Wz", r, r + 128), B("zl", z0, z0 + p[3]), st, alone or (not st and p is ps[-1]))]))
-
-        for h, (c0, c1, e, eo, pa, ao) in enumerate(CH):
+        razor = par and t < STEPS - 1
+        if razor:
+            xtake(t // 2, 0)
+        for b in range(2):
+            e = "pE%d" % b
+            PE(512, ET + ["phm%d_0" % t, "phm%d_1" % t], [e],
+               mms([(B(e, j, H, 8), B("E", 128 * j, 128 * j + 128), B("phm", 2 * o + 56 * b, 2 * o + 56 * b + 56), True, True) for j in range(8)]))
+        for h, (c0, c1, bank, mode, _ways) in enumerate(CH[t]):
             n, j0 = 16 * (c1 - c0), 16 * c0
-            s0, ah, dh, eh = K * t + j0, B("a", j0, j0 + n), B("d", j0, j0 + n), B(e, eo, eo + n)
-            PE(512, ["E8", "phi%d_0" % t, "phi%d_1" % t], [e],
-               mms([(B(e, eo + j, eo + n, 8), B("E8", 128 * j, 128 * j + 128), B("phi", 112 * t + 2 * c0, 112 * t + 2 * c1), True, True) for j in range(8)]))
-            if t and not ZLAST[par][h]:
-                zmm(h, True)
-            S(n, wt + ["offv%d" % t], ["a%d" % h], act(ah, G(win, L, "offv", o + c0, o + c1), F.Copy), "g")
-            V(n, wt + ["offw%d" % t, "a%d" % h], ["d%d" % h], tt(dh, G(win, L + 1, "offw", o + c0, o + c1), ah, A.subtract), "t")
-            if h in LATE.get(t, ()):
-                V(n, ["d%d" % h, e], ["d%d" % h], tt(dh, dh, eh, A.mult))
-                if t + 1 < STEPS:
-                    V(n, ["a%d" % h, "d%d" % h], ["s%d_%d" % (t, h)], tt(B("s", s0, s0 + n), ah, dh, A.add), 2.0)
+            e, s0 = "pE%d" % (c0 // 28), K * t + j0
+            ah, dh, sh, eh = B("a", s0, s0 + n), B("d", j0, j0 + n), B("s", s0, s0 + n), B(e, j0 % H, j0 % H + n)
+            at, st, dt = "a%d_%d" % (t, h), "s%d_%d" % (t, h), quarters("d", c0, c1)
+            S(n, wt + ["offv%d" % t], [at], act(ah, G(win, L + over(t), "offv", o + c0, o + c1), F.Copy), "g")
+            V(n, wt + ["offw%d" % t, at], dt, tt(dh, G(win, L + over(t) + 1, "offw", o + c0, o + c1), ah, A.subtract), "t")
+            if mode in "wf":
+                V(n, dt + [e], [st], tt(sh, dh, eh, A.mult))
             else:
-                V(n, ["d%d" % h, e], [e], tt(eh, dh, eh, A.mult))
-                V(n, ["a%d" % h, e], ["s%d_%d" % (t, h)], tt(B("s", s0, s0 + n), ah, eh, A.add))
-            for x in ops[-4:]:
-                x["lead"] = -LEAD * h
+                V(n, dt + [e], [e], tt(eh, dh, eh, A.mult))
+                V(n, [at, e], [st], tt(sh, ah, eh, A.add))
             if t + 1 < STEPS:
                 ps = [p for p in pieces(t) if p[0] == h]
-                rd = "s%d_%d" % (t, h)
-                if t in CODE:
-                    V(n, [rd], ["c" + rd], ts(B("s16", s0, s0 + n), B("s", s0, s0 + n), CODE[t], None, A.mult))
-                    rd = "c" + rd
-                send("z", (t, h), [rd], {p[4]: p[4] for p in ps}, (256 if t in CODE else 512) * ps[0][3], {p[4]: p[1] for p in ps})
-        for h, (c0, c1, e, eo, pa, ao) in enumerate(CH):
+                send("z", (t, h), [st] + [at] * (mode == "w"), {p[4]: p[4] for p in ps}, 512 * ps[0][3], {p[4]: p[1] for p in ps},
+                     2 if mode == "w" else 1)
+        for h, (c0, c1, bank, mode, _ways) in enumerate(CH[t]):
             n, j0 = 16 * (c1 - c0), 16 * c0
-            s0, out = K * t + j0, B("X", par + 2 * j0, 2 * (j0 + n), 2)
-            if t == 0:
-                S(n, ["s0_%d" % h], ["X0%d" % h], act(out, B("s", s0, s0 + n), F.Tanh, scale=0.625))
-                if h == 0:
-                    S(1, ["s0_0"], ["Xm"], act(B("X", L, L + 1), B("s", 0, 1), F.Tanh, scale=0.625))
-                continue
-            ph = B(pa, ao, ao + n)
-            if h in LATE.get(t, ()):
-                zl = ZLAST[par][h]
-                PE(4 * n, ["Wi", "a%d" % h], [pa], mms([(ph, B("Wi", 0, 128), B("a", j0, j0 + n), zl, False)]))
-                PE(4 * n, ["Wi", "d%d" % h], [pa], mms([(ph, B("Wi", 0, 128), B("d", j0, j0 + n), False, not zl)]))
-                if zl:
-                    zmm(h, False)
-            elif ADD[par][h] == "v":
-                if ZLAST[par][h]:
-                    zmm(h, True)
-                V(n, ["s%d_%d" % (t, h), pa], [pa], tt(ph, B("s", s0, s0 + n), ph, A.add))
-            else:
-                PE(4 * n, ["Wi", "s%d_%d" % (t, h)], [pa], mms([(ph, B("Wi", 0, 128), B("s", s0, s0 + n), ZLAST[par][h], not ZLAST[par][h])]))
-                if ZLAST[par][h]:
-                    zmm(h, False)
-            S(n, [pa], ["X%d%d" % (par, h)], act(out, ph, F.Tanh, scale=0.625))
-            if par == 0 and h == 0:
-                S(1, [pa], ["Xm"], act(B("X", L, L + 1), B(pa, ao, ao + 1), F.Tanh, scale=0.625))
+            pa, s0 = "pA%d" % bank, K * t + j0
+            sh, ph, out = B("s", s0, s0 + n), B(pa, 0, n), B("X", par + 2 * j0, 2 * (j0 + n), 2)
+            at, st, xt = "a%d_%d" % (t, h), "s%d_%d" % (t, h), quarters("X%d" % par, c0, c1)
+            own = mode in "wpf"
+            terms = [(["Wi", at], ph, B("Wi", 0, 128), B("a", s0, s0 + n), n) if mode in "wf" else (["Wi", st], ph, B("Wi", 0, 128), sh, n)] * own
+            if t:
+                r = 16 * (t % 8)
+                ps = [(max(p[2], j0), min(p[2] + p[3], j0 + n), p[4]) for p in pieces(t - 1)]
+                ps = [p for p in ps if p[0] < p[1]]
+                if own and not ZLAST[par]:
+                    terms = [(["Wz"] + [p[2] for p in ps], ph, B("Wz", r, r + 128), B("zl", s0 - K, s0 - K + n), n)] + terms
+                else:
+                    terms = terms + [(["Wz", z], B(pa, a - j0, b - j0), B("Wz", r, r + 128),
+                                      B("zl", K * (t - 1) + a, K * (t - 1) + b), b - a) for a, b, z in ps]
+            if mode == "f":
+                terms = terms + [(["Wi", st], ph, B("Wi", 0, 128), sh, n)]
+            for i, (rd, po, lt, rh, w) in enumerate(terms):
+                if t % 8 == 0 and mode == "u":
+                    S(w, rd[1:], [pa], act(po, rh, F.Copy, scale=0.6))
+                else:
+                    PE(4 * w, rd, [pa], mms([(po, lt, rh, i == 0 or not own, i == len(terms) - 1 or not own)]))
+            src, tok = ph, [pa]
+            if kept(t):
+                src, tok = B("arg", par + 2 * j0, 2 * (j0 + n), 2), quarters("arg%d" % par, c0, c1)
+            if mode == "s":
+                src, tok = sh, [st]
+            elif mode not in "pf":
+                V(n, [st, pa], tok, tt(src, sh, ph, A.add))
+            S(n, tok, xt, act(out, src, F.Tanh, scale=0.625))
+            if par == 0 and c0 == 0:
+                S(17, ["X00", "X10"], ["Xm"], act(B("X", L, L + 17), B("X", 0, 17), F.Copy))
             if t == STEPS - 1:
-                dma("sync", "st", 1024 * (j0 + n), ["X0%d" % h, "X1%d" % h], [],
+                dma("st", 1024 * n, quarters("X0", c0, c1) + xt, [],
                     lambda g, T, j0=j0, n=n: g.sync.dma_start(T.yx[:, 2 * j0:2 * (j0 + n)], T.X[:, 2 * j0:2 * (j0 + n)]))
         if razor:
-            m = t // 2
-            if XEARLY:
-                xtake(m, 1, 1)
-                xput(m, 0, 1)
-                xput(m, 1, 1)
-            else:
-                xtake(m, 0, 2)
-                xput(m, 0, 2)
+            xtake(t // 2, 1)
+            xput(t // 2, 0)
+            xput(t // 2, 1)
 
     lists(0)
     for t in range(STEPS):
-        part[:] = ["c%d" % (t % 2), 0]
+        part[0] = "c%d" % t
         cstep(t)
         if t % 2 == 1 and t < STEPS - 1:
+            part[0] = "cr%d" % t
             crazor(t // 2)
-    part[:] = ["e", 0]
-    PE(16 * 112, ["W8"] + DA, ["pR"],
-       mms([(B("pR", 0, 112), B("W8", 15 - j, 143 - j), B("D", 112 * j, 112 * j + 112), j == 0, j == 15) for j in range(16)]))
-    V(112, ["pR"], ["ycf"], ts(B("ycf"), B("pR", 0, 112), 128.0, None, A.add))
-    dma("sync", "st", 0, ["ycf"], [], lambda g, T: g.sync.dma_start(T.yc[:], T.ycf[:]))
-    V(56, ["P"], ["Pi"], ts(B("Pi"), B("P"), 128.0 * STEPS, None, A.add))
+    part[0] = "e"
+    for p in range(2):
+        PE(1024, ["Wh"] + DA[2 * p:2 * p + 2], ["pR"],
+           tracks(B("pR", p, 112, 2), "Wh", lambda j, p=p: B("D", 112 * j + p, 112 * j + 112, 2), True, True))
+    V(112, ["pR"], ["ycf"], ts(B("ycf"), B("pR", 0, 112), 16.0, 128.0, A.mult, A.add))
+    dma("st", 0, ["ycf"], [], lambda g, T: g.sync.dma_start(T.yc[:], T.ycf[:]))
+    V(56, [wrapped[1]], ["Pi"], ts(B("Pi"), wrapped[0], 16.0, 16.0 * drift(STEPS) + 7.5, A.mult, A.add))
     V(56, ["Pi"], ["yp0"], ts(B("ypi", 0, 56), B("Pi"), 8, None, A.arith_shift_right))
     V(56, ["Pi"], ["yp1"], ts(B("ypi", 56, 112), B("Pi"), 255, None, A.bitwise_and))
     V(112, ["yp0", "yp1"], ["ypf"], cp(B("ypf"), B("ypi")))
-    dma("sync", "st", 0, ["ypf"], [], lambda g, T: g.sync.dma_start(T.yp[:], T.ypf[:]))
+    dma("st", 0, ["ypf"], [], lambda g, T: g.sync.dma_start(T.yp[:], T.ypf[:]))
     for t in range(STEPS):
-        part[:] = ["x%s" % (t % 2 if 0 < t < STEPS - 1 else "ab"[t % 2]), 0]
+        part[0] = "x%d" % t
         xstep(t)
     return ops
 
 
-def order(ops):
+def depend(ops):
     lastw, readers, arrival = {}, {}, {}
     for i, o in enumerate(ops):
         dep, arr = set(), []
@@ -431,131 +443,55 @@ def order(ops):
         for k, sem in o.get("arr", {}).items():
             arrival[k] = (i, sem)
         o["dep"], o["wait_arr"] = sorted(dep), arr
-    return rank_calls(ops)
 
 
-def rank_calls(ops):
-    n = len(ops)
-    pre = [set(o["dep"]) | set(j for j, _s in o["wait_arr"]) for o in ops]
-    suc = [[] for _ in ops]
-    for i in range(n):
-        for j in pre[i]:
-            suc[j].append(i)
-    prio = [0.0] * n
-    M = MODEL
-    for i in range(n - 1, -1, -1):
-        ops[i]["dur"], ops[i]["lat"] = cost(ops[i], M)
-        far = max(land(ops[i], 0.0, M, {}).values()) if "send" in ops[i] else 0.0
-        prio[i] = ops[i]["dur"] + ops[i]["lat"] + far + max([prio[j] + M["sem"] for j in suc[i]], default=0.0)
-    for i in range(n):
-        a, b = ops[i]["cls"]
-        prio[i] += (AHEAD if a[0] in "ci" else 0.0) + (0.5 * (ord(SHIFT[a][b]) - 77) if b < len(SHIFT.get(a, "")) else 0.0) + ops[i].get("lead", 0.0) + (1000.0 * (100 - i) if ops[i]["q"] in ("sync", "pool") and not pre[i] else 0.0)
-    left = [len(p) for p in pre]
-    ready = {i: 0.0 for i in range(n) if not left[i]}
-    free, seq, end, landed, busy = {}, [], 0.0, {}, {}
-    while ready:
-        st = {i: max(r, free.get(ops[i]["q"], 0.0)) for i, r in ready.items()}
-        b = min(st, key=lambda i: (st[i], -prio[i]))
-        c = max((i for i in st if ops[i]["q"] == ops[b]["q"] and st[i] <= st[b] + SLACK), key=lambda i: prio[i])
-        o = ops[c]
-        o["start"] = st[c]
-        free[o["q"]] = st[c] + o["dur"]
-        o["done"] = st[c] + o["dur"] + o["lat"]
+def plain(tok):
+    head = tok.rstrip("0123456789")
+    if head == "arg":
+        return head + tok[-1]
+    if head in ("X", "D", "cf", "pE", "pA", "pT", "cg", "sg", "d", "acc", "own", "E", "ci", "yp", "W", "c", "I"):
+        return tok
+    i = [j for j, c in enumerate(tok + "0") if c.isdigit()][0]
+    return tok[:i] + tok[i:].lstrip("0123456789")
+
+
+def arrange(ops):
+    place, seen, queues = {}, {}, {q: [] for q in ORDER}
+    for q, text in ORDER.items():
+        for r, w in enumerate(text.split()):
+            name, _, back = w.partition("@")
+            place[q, name] = (int(back or 0), r)
+    for i, o in enumerate(ops):
+        p = o["cls"][0]
+        rnd = {"i": 0, "e": NR}[p] if p in ("i", "e") else int(p[-1]) // 2
+        if p[0] in "cx":
+            p = "r" if p[1] == "r" else p[0] + "eo"[int(p[-1]) % 2]
+            p = p if p == "r" or 0 < rnd < NR else p + "0" if rnd == 0 else p.upper()
         if "send" in o:
-            landed.update(land(o, o["done"], M, busy))
-        end = max(end, o["done"])
-        seq.append(c)
-        del ready[c]
-        for j in suc[c]:
-            left[j] -= 1
-            if not left[j]:
-                ready[j] = max([ops[k]["done"] + (0.0 if ops[k]["q"] == ops[j]["q"] == "pe" else M["sem"]) for k in ops[j]["dep"]]
-                               + [landed[s] + M["sem"] for _k, s in ops[j]["wait_arr"]])
-    return seq, end
-
-
-def polish(ops, seq, rounds):
-    n = len(ops)
-    qs = [o["q"] for o in ops]
-    ms = [dict(MODEL, **x) for x in SPREAD]
-    co = [[cost(o, M) for o in ops] for M in ms]
-    dep = [[(j, qs[j] == o["q"] == "pe") for j in o["dep"]] for o in ops]
-    pre = [set(o["dep"]) | set(j for j, _s in o["wait_arr"]) for o in ops]
-    arr = [o["wait_arr"] for o in ops]
-    snd = ["send" in o for o in ops]
-
-    def run(sq, m, p0, old):
-        M, c, sm = ms[m], co[m], ms[m]["sem"]
-        done, rel, why, landed, snap = (list(old[0]), list(old[1]), list(old[2]), dict(old[3]), dict(old[4])) if old else ([0.0] * n, [0.0] * n, [0] * n, {}, {})
-        last, busy = {}, {}
-        for i in sq[:p0]:
-            last[qs[i]] = i
-            if snd[i]:
-                busy = snap[i]
-        busy = dict(busy)
-        for i in sq[p0:]:
-            w = last.get(qs[i], -1)
-            s = rel[w] if w >= 0 else 0.0
-            w = -2 - w
-            for j, p in dep[i]:
-                x = done[j] if p else done[j] + sm
-                if x > s:
-                    s, w = x, j
-            for j, a in arr[i]:
-                if landed[a] + sm > s:
-                    s, w = landed[a] + sm, j
-            rel[i] = s = s + c[i][0]
-            done[i] = s + c[i][1]
-            why[i] = w
-            last[qs[i]] = i
-            if snd[i]:
-                landed.update(land(ops[i], s, M, busy))
-                snap[i] = dict(busy)
-        return done, rel, why, landed, snap, max(done)
-
-    rng = np.random.default_rng(7)
-    st = [run(seq, m, 0, None) for m in range(len(ms))]
-    cur = best = sum(x[5] for x in st)
-    keep = seq
-    for r in range(rounds):
-        s = st[r % len(ms)]
-        i, arcs = s[0].index(s[5]), []
-        while s[2][i] != -1:
-            w = s[2][i]
-            if w < -1:
-                w = -2 - w
-                if w not in pre[i] and qs[i] != "sync":
-                    arcs.append((w, i))
-            i = w
-        u, v = arcs[int(rng.integers(len(arcs)))]
-        pu, pv = seq.index(u), seq.index(v)
-        need, needq, want = [v], set(), set(pre[v])
-        for x in reversed(seq[pu + 1:pv]):
-            if x in want or qs[x] in needq:
-                need.append(x)
-                needq.add(qs[x])
-                want |= pre[x]
-        if u in want:
-            continue
-        ns = set(need)
-        sq = seq[:pu] + need[::-1] + [x for x in seq[pu:pv] if x not in ns] + seq[pv + 1:]
-        new = [run(sq, m, pu, st[m]) for m in range(len(ms))]
-        val = sum(x[5] for x in new)
-        if val < cur + HEAT * (1.0 - r / rounds) * float(rng.exponential()):
-            seq, st, cur = sq, new, val
-            if val < best:
-                best, keep = val, sq
-    done = run(keep, 0, 0, None)[0]
-    for i in range(n):
-        ops[i]["done"] = done[i]
-    return keep
+            name = "send" + o["send"][0] + plain(o["rd"][0])
+        elif not o["wr"]:
+            name = "st" + plain(o["rd"][0])
+        else:
+            name = plain(o["wr"][0]) + ("<" + ("E" if o["rd"][1][0] == "E" else plain(o["rd"][1])) if o["q"] == "pe" else "")
+        name = p + "." + name
+        seen[o["q"], name, rnd] = seen.get((o["q"], name, rnd), -1) + 1
+        back, r = place[o["q"], name + "'" * seen[o["q"], name, rnd]]
+        queues[o["q"]].append((rnd + back, r, i))
+    queues = [sorted(v, reverse=True) for v in queues.values()]
+    seq, done = [], set()
+    while len(seq) < len(ops):
+        for v in queues:
+            while v and all(j in done for j in ops[v[-1][2]]["dep"] + [x[0] for x in ops[v[-1][2]]["wait_arr"]]):
+                seq.append(v.pop()[2])
+                done.add(seq[-1])
+    return seq
 
 
 def helpers(T, topo):
     place = lambda c: (topo.host(c), topo.chip(c))
     busy = set(place(c) for c in T.cores)
     used, out = set(), {}
-    names = sorted(set(w for v in ROUTE.values() for ws in v for w in ws if w != "D"))
+    names = sorted(set(w for v in CH[:-1] for c in v for w in c[4] if w != "D"))
     n = len(T.cores)
     for w in names:
         for r, c in enumerate(T.cores):
@@ -576,6 +512,16 @@ def bits(es):
     return sum(1 << e for e in es)
 
 
+def hop_engines(T, topo, hp, r, t, p):
+    c = T.cores[r]
+    far = topo.engines(c, T.cores[(r + 1) % len(T.cores)])
+    mine = [x for x in pieces(t) if x[0] == p[0] and (x[1][0] == "A") == (p[1][0] == "A")]
+    pool = far if p[1][0] != "A" else [e for e in topo.engines(c, hp[r, p[1]]) if e not in far]
+    k = len(pool) // len(mine)
+    i = mine.index(p)
+    return pool[i * k:(i + 1) * k]
+
+
 PLAN = {}
 
 
@@ -584,8 +530,8 @@ def rank_program(g, core, T, topo):
     n = len(T.cores)
     if "seq" not in PLAN:
         PLAN["ops"] = build()
-        PLAN["seq"], PLAN["end"] = order(PLAN["ops"])
-        PLAN["seq"] = polish(PLAN["ops"], PLAN["seq"], ROUNDS)
+        depend(PLAN["ops"])
+        PLAN["seq"] = arrange(PLAN["ops"])
         PLAN["help"] = helpers(T, topo)
     ops, hp = PLAN["ops"], PLAN["help"]
     if rank is None:
@@ -595,14 +541,13 @@ def rank_program(g, core, T, topo):
                 continue
             d = T.cores[(r + 1) % n]
             rid, pid = topo.addr(d, core)
-            ne = len(topo.engines(core, d))
             for t in range(STEPS - 1):
                 for p in pieces(t):
                     if p[1] == w:
-                        ap = T["z16" if t in CODE else "zl"][:, K * t + p[2]:K * t + p[2] + p[3]]
-                        g.wait_ge(T.sem[p[4]], first_hop(T, topo, hp, r, t, p))
+                        ap = T.zl[:, K * t + p[2]:K * t + p[2] + p[3]]
+                        g.wait_ge(T.sem[p[4]], len(hop_engines(T, topo, hp, r, t, p)))
                         g.remote_dma(ap, ap, T.sem[p[4]], T.sem.sent, pid, rid, topo.mask(core, d))
-                        sent += ne
+                        sent += len(topo.engines(core, d))
         if sent:
             g.wait_ge(T.sem.sent, sent)
         return
@@ -617,7 +562,7 @@ def rank_program(g, core, T, topo):
             for p in pieces(t):
                 if p[4] == sem:
                     if p[1] == "D":
-                        return first_hop(T, topo, hp, prv, t, p)
+                        return len(hop_engines(T, topo, hp, prv, t, p))
                     return len(topo.engines(hp[prv, p[1]], core))
         return len(topo.engines(T.cores[prv], core))
 
@@ -629,36 +574,32 @@ def rank_program(g, core, T, topo):
                 known[q][k] = max(known[q].get(k, 0), v)
 
     def remote(kind, key):
-        rid, pid = topo.addr(nxt, core)
-        if kind == "c":
-            g.remote_dma(T.lc[:, PC * key:PC * key + PW], T.pc[:, PC * key:PC * key + PW], T.sem["rc%d" % key], T.sem.sent, pid, rid, bits(far))
+        if kind != "z":
+            (rid, pid), (b, w, sem) = topo.addr(nxt, core), key
+            g.remote_dma(T["l" + kind][:, b:b + w], T["p" + kind][:, b:b + w], T.sem[sem], T.sem.sent, pid, rid, bits(far))
             sent[0] += len(far)
-        elif kind == "x":
-            b, w, sem = key
-            g.remote_dma(T.lx[:, b:b + w], T.px[:, b:b + w], T.sem[sem], T.sem.sent, pid, rid, bits(far))
-            sent[0] += len(far)
-        else:
-            t, h = key
-            trs = []
-            for p in pieces(t):
-                if p[0] == h:
-                    d = nxt if p[1] == "D" else hp[rank, p[1]]
-                    r2, p2 = topo.addr(d, core)
-                    es = hop_engines(T, topo, hp, rank, t, p)
-                    a = K * t + p[2]
-                    trs.append(RemoteDMATransfer(dst_ids=[DstId(rid=r2, pnc=p2)], dma_engine_mask=bits(es), remote_sem=T.sem[p[4]],
-                                                 src=T["s16" if t in CODE else "s"][:, a:a + p[3]],
-                                                 dst=T["z16" if t in CODE else "zl"][:, a:a + p[3]]))
-                    sent[0] += len(es)
-            g.remote_dma_fused(trs, local_sem=T.sem.sent)
+            return
+        t, h = key
+        trs = []
+        for p in pieces(t):
+            if p[0] == h:
+                rid, pid = topo.addr(nxt if p[1] == "D" else hp[rank, p[1]], core)
+                es = hop_engines(T, topo, hp, rank, t, p)
+                a, b = K * t + p[2], K * t + p[2] + p[3]
+                how = dict(src=T.s[:, a:b], dst=T.zl[:, a:b])
+                if CH[t][h][3] == "w":
+                    how = dict(srcs=[T.a[:, a:b], T.s[:, a:b]], dsts=[T.zl[:, a:b]], alu_op=1)
+                trs.append(RemoteDMATransfer(dst_ids=[DstId(rid=rid, pnc=pid)], dma_engine_mask=bits(es), remote_sem=T.sem[p[4]], **how))
+                sent[0] += len(es)
+        g.remote_dma_fused(trs, local_sem=T.sem.sent)
 
+    at = {i: r for r, i in enumerate(PLAN["seq"])}
     for i in PLAN["seq"]:
         o = ops[i]
         q = o["q"]
         need = [j for j in o["dep"] if not (q == "pe" and ops[j]["q"] == "pe")]
-        for j in sorted(need, key=lambda j: -ops[j]["done"]):
-            sem, val, more = clock[j]
-            wait(q, sem, val, more)
+        for j in sorted(need, key=lambda j: -at[j]):
+            wait(q, *clock[j])
         for _j, sem in o["wait_arr"]:
             wait(q, sem, arrives(sem), {})
         if "send" in o:
@@ -671,17 +612,3 @@ def rank_program(g, core, T, topo):
     for sem, val in count.items():
         wait("pool", sem, val, {})
     g.wait_ge(T.sem.sent, sent[0])
-
-
-def hop_engines(T, topo, hp, r, t, p):
-    c = T.cores[r]
-    far = topo.engines(c, T.cores[(r + 1) % len(T.cores)])
-    mine = [x for x in pieces(t) if x[0] == p[0] and (x[1][0] == "A") == (p[1][0] == "A")]
-    pool = far if p[1][0] != "A" else [e for e in topo.engines(c, hp[r, p[1]]) if e not in far]
-    k = len(pool) // len(mine)
-    i = mine.index(p)
-    return pool[i * k:(i + 1) * k]
-
-
-def first_hop(T, topo, hp, r, t, p):
-    return len(hop_engines(T, topo, hp, r, t, p))

from concourse.bass import DstId, RemoteDMATransfer
from concourse.mybir import AluOpType, ActivationFunctionType

A = AluOpType
F = ActivationFunctionType
L, K, H, STEPS, NR, WORLD = 1792, 896, 448, 10, 4, 256
LC = 62
SRC = 32 * LC
GATE = 2048
XW = SRC + GATE
PW, PC = 204, 208

FIRST = [(0, 28, 0, "s", ["A0", "B0"]), (28, 56, 1, "s", ["D"])]
EVEN = [(0, 28, 0, "p", ["A0", "B0"]), (28, 56, 1, "v", ["D"])]
ODD = [(0, 28, 0, "w", ["A0", "A1"]), (28, 56, 1, "v", ["D"])]
EIGHTH = [(0, 14, 0, "p", ["A0", "B0"]), (28, 42, 1, "u", ["D"]), (14, 28, 0, "p", ["D"]), (42, 56, 1, "u", ["D"])]
LAST = [(0, 14, 0, "w", []), (28, 42, 1, "w", []), (14, 28, 0, "w", []), (42, 56, 1, "w", [])]
CH = [FIRST, ODD] + [EVEN, ODD] * 3 + [EIGHTH, LAST]
ZLAST = {0: False, 1: True}
CG = ["av", "aa"] * 5

ORDER = {
    "pe": """e.pR<D00@1 CO.pS<Iw@1 CE.pS<P e.pR<D10@1 XE.pE0<E XE.pE1<E CE.pT0<D00 ce.pT1<D01 ce.pT0<D00 ce.pT1<cg1 ce.pT0<cg0
        ce.pS<P ce.pS<cg0 co.pR<D10 ce0.pS<P co.pT1<D11 CE.pT1<D01 CE.pT1<cg1 ce0.pT0<rawc ce0.pT1<rawc ce0.pT0<cg0 ce0.pT1<cg1
        ce0.pS<cg0 i.pR<sel xe.pE1<E xe.pE0<E co.pT0<D10 xe.pA1<z_2 xe.pA0<z_0 co.pT1<cg1 co.pT0<cg0 CE.pS<cg0 XE.pA0<z_0
        XE.pA0<s_0 CE.pT0<cg0 xe.pA0<s_0 co.pR<cg0 co0.pT0<D10 xe0.pE1<E co0.pT1<D11 xe0.pE0<E co0.pR<D10 co0.pT1<cg1 co0.pS<P
        co0.pT0<cg0 co.pR<sg0 co0.pR<cg0 co0.pR<sg0 co0.pS<cg0 xo.pE0<E r.pR<Bm xo.pE1<E co.pS<P CO.pS<P XE.pA0<z_1 XE.pA0<s_2
        XO.pE0<E XO.pE1<E CO.pT0<D10 XO.pA1<a_1 XO.pA1<z_2 XO.pA0<a_0 CO.pT1<D11 XO.pA0<z_0 CO.pT0<cg0 XO.pA0<z_1 XO.pA1<a_3
        XO.pA1<z_4 CO.pT1<cg1 XO.pA0<a_2 XO.pA0<z_3 CO.pS<cg0 co.pS<cg0 xo.pA0<a_0 xo0.pA0<a_0 xo0.pE0<E r.pR<acc1 r.pR<fl
        xo.pA0<z_0 xo0.pE1<E co0.pS<Iw xo0.pA1<z_2 xo0.pA0<z_0 xo.pA0<z_1 xo.pA1<z_2 co.pS<Iw xo0.pA0<z_1""",
    "dve": """xo.s_1@1 xo.arg0@1 xo.arg2@1 co.offv@1 r.dst@1 co.vf@1 xo0.arg0@1 r.D00@1 co0.vf@1 XO.pA1'@1 XO.s_2@1 CO.D11@1 XO.pA0'@1
        CO.D10@1 e.Pi@1 i.ci2 i.ci3 i.ci4 i.ci1 i.cf i.Wi i.cf5 i.kcol i.Wh i.cf8 i.cf6 i.P i.offv co.phi@1 ce.cg1 co0.phi@1
        xo0.X00@1 i.E0 i.cf7 i.keep i.E3 i.vf xo.X00@1 i.phi i.E1 i.E2 i.sel ce0.cg1 i.thb i.D10 i.offw e.yp1@1 e.yp0@1 ce.D01
        co.offw@1 CE.cg1 e.ypf@1 e.ycf@1 ce.D00 XE.d2 XE.d0 XE.pE1 XE.pE0 XE.s_1 XE.d1 XE.s_0 XE.d3 XE.pE0' ce.offv ce.vf
        co0.offw@1 ce.phi i.Bm i.rawm ce0.D00 ce0.offv i.thc ce0.D01 xe0.d0 ce0.vf xe0.pE0 xe0.d2 xe0.s_0 xe0.pE1 xe.d0 xe.d2
        xe.pE0 xe.s_0 xe.pE1 xe.s_1 xe0.s_1 ce0.phi CE.offv XE.pA1 XE.s_2 CE.vf XE.pE1' CE.phi XE.s_3 XE.pA1' CE.D00 CE.offw
        CE.D01 xe.pA1 ce.offw co.D10 co.D11 XO.d3 XO.d2 XO.d1 XO.s_1 XO.d0 XO.pA1 XO.s_0 XO.pA0 co0.D11 ce0.offw r.cum co0.D10
        xo.d0 xo0.d0 r.colk r.fl xo0.s_0 xo.s_0 xo.d2 xo0.d2 r.src_0 xo.pE1 XO.s_3 xo0.pE1 xo0.s_1 co0.offv r.y xo0.arg2""",
    "act": """xo0.pxe@1 CO.sg1@1 XO.X13@1 CO.sg0@1 CO.P@1 CO.wr@1 XO.X11@1 xo0.X12@1 xo0.pxo@1 xo.pxo@1 xo.X10@1 xo.X12@1 i.Dd i.c8
        i.argd i.Wz i.I8 i.kcol i.Wn i.cut i.Ib ce0.cg0 xo0.X10@1 ce.cg0 co0.phm_0@1 co.phm_1@1 co.phm_0@1 co0.phm_1@1 ce.sg1
        xo.Xm@1 xo0.Xm@1 ce.sg0 xo.X00@1 xo0.X00@1 ce.P XE.a_1 XE.a_0 CE.cg0 XE.a_2 XE.pA1 XE.a_3 xe.a_0 xe.a_1 ce.Dd co.cg1
        co.cg0 CE.P CE.sg1 i.phm_1 i.phm_0 i.W2 ce0.sg0 ce0.sg1 ce0.P xe0.a_0 ce0.Dd xe0.a_1 co0.cg1 co0.cg0 co0.sg1 co0.sg0
        xe0.X00 i.Iw ce.phm_1 co.sg1 co.sg0 ce.phm_0 xe.X00 XE.X00 CE.sg0 XE.X02 XE.pA1' XE.Xm XE.X01 CE.phm_1 XE.X03 CE.phm_0
        xe.Xm xe.X02 xe0.Xm r.cut xe0.X02 ce0.phm_1 xo0.a_0 xo.a_0 XO.a_3 XO.a_1 XO.a_2 XO.a_0 CE.Dd CO.cg0 XO.X12 CO.cg1 XO.X10
        ce0.phm_0 r.acc3 r.acc4 r.acc2 r.acc5 r.acc1 r.acc0 r.pg xo0.a_1 co0.wr co0.P xo.a_1 co.P co.wr r.own0 r.own1 r.pc
        xo.pxe""",
    "pool": """r.sendcpc@1 xo.sendxpxe@1 i.xr i.ci0 i.xe i.Xd xo0.sendxpxe@1 xo.sendxpxo@1 xo0.sendzs_1@1 xo0.sendxpxo@1 xo.sendzs_1@1
        i.arg0 i.X10 i.Lm i.Um xe.sendzs_0 XE.sendzs_0 XE.sendzs_1 xe0.sendzs_0 xe.sendzs_1 XE.sendzs_3 XE.sendzs_2 xe0.sendzs_1
        r.sendcpg xo.sendzs_0 xo0.sendzs_0""",
    "sync": """XO.stX02@1 XO.stX00@1 i.posi i.rawc i.thi i.rawx XO.stX03@1 XO.stX01@1 e.stypf@1 e.stycf@1""",
}

SCRATCH = {
    "rawx": ("sbuf", [128, L + 16], "bfloat16"), "rawc": ("sbuf", [128, L], "bfloat16"),
    "X": ("sbuf", [128, XW], "float32"), "D": ("sbuf", [128, XW], "bfloat16"), "arg": ("sbuf", [128, SRC], "float32"),
    "posi": ("sbuf", [128, 56], "int32"), "P": ("sbuf", [128, 56], "float32"), "wr": ("sbuf", [128, 56], "bfloat16"),
    "Pi": ("sbuf", [128, 56], "int32"), "vf": ("sbuf", [128, 56], "float32"),
    "offv": ("sbuf", [128, 560], "uint16"), "offw": ("sbuf", [128, 560], "uint16"),
    "phi": ("sbuf", [128, 560], "bfloat16"), "phm": ("sbuf", [128, 1120], "bfloat16"),
    "cg": ("sbuf", [128, K], "bfloat16"), "sg": ("sbuf", [128, K], "bfloat16"),
    "a": ("sbuf", [128, K * STEPS], "float32"), "d": ("sbuf", [128, K], "float32"),
    "s": ("sbuf", [128, K * STEPS], "float32"), "zl": ("sbuf", [128, K * (STEPS - 1)], "float32"),
    "pc": ("sbuf", [128, PC * NR], "bfloat16"), "lc": ("sbuf", [128, PC * NR], "bfloat16"),
    "px": ("sbuf", [128, 192 * NR], "float32"), "lx": ("sbuf", [128, 192 * NR], "float32"),
    "srcl": ("sbuf", [128, 12 * NR], "uint16"), "dstl": ("sbuf", [128, 12 * NR], "uint16"),
    "cut": ("sbuf", [128, LC + 2], "bfloat16"), "cum": ("sbuf", [128, 128], "float32"),
    "junk": ("sbuf", [128, 6 * 64], "bfloat16"), "acc": ("sbuf", [128, 6], "float32"), "colk": ("sbuf", [128, 6], "uint16"),
    "fl": ("sbuf", [128, 96], "bfloat16"), "own": ("sbuf", [128, 12], "float32"), "y12": ("sbuf", [128, 12], "float32"),
    "thi": ("sbuf", [128, 4], "int32"), "thb": ("sbuf", [128, 4], "bfloat16"), "thc": ("sbuf", [128, 4], "float32"),
    "ci": ("sbuf", [128, 8], "int32"), "cf": ("sbuf", [128, 12], "float32"),
    "xr": ("sbuf", [128, 256], "float32"), "xe": ("sbuf", [128, 256], "bfloat16"),
    "Wi": ("sbuf", [128, 256], "float32"), "Wz": ("sbuf", [128, 256], "float32"), "Ib": ("sbuf", [128, 128], "bfloat16"),
    "Wh": ("sbuf", [128, 144], "bfloat16"), "W2": ("sbuf", [128, 144], "bfloat16"), "Wn": ("sbuf", [128, 144], "bfloat16"),
    "E": ("sbuf", [128, 1024], "bfloat16"),
    "Bm": ("sbuf", [128, 128], "bfloat16"), "Lm": ("sbuf", [128, 128], "bfloat16"), "Um": ("sbuf", [128, 128], "bfloat16"),
    "sel": ("sbuf", [128, 128], "bfloat16"), "keep": ("sbuf", [128, 128], "float32"), "c8": ("sbuf", [128, 128], "bfloat16"),
    "Iw": ("sbuf", [128, 128], "bfloat16"), "I8": ("sbuf", [128, 128], "bfloat16"),
    "kcol": ("sbuf", [128, 12], "float32"),
    "ypi": ("sbuf", [128, 112], "int32"), "ypf": ("sbuf", [128, 112], "float32"), "ycf": ("sbuf", [128, 112], "float32"),
    "pE0": ("psum", [128, 512], "float32"), "pE1": ("psum", [128, 512], "float32"),
    "pA0": ("psum", [128, 512], "float32"), "pA1": ("psum", [128, 512], "float32"),
    "pT0": ("psum", [128, 512], "float32"), "pT1": ("psum", [128, 512], "float32"),
    "pS": ("psum", [128, 512], "float32"), "pR": ("psum", [128, 512], "float32"),
}
BANKS = ("pE0", "pE1", "pA0", "pA1", "pT0", "pT1", "pS", "pR")


def pieces(t):
    out = []
    for h, c in enumerate(CH[t]):
        n = 16 * (c[1] - c[0]) // len(c[4])
        for i, w in enumerate(c[4]):
            out.append((h, w, 16 * c[0] + i * n, n, "z%d_%d" % (t, len(out))))
    return out


SEMAPHORES = (["pe", "dve", "act", "pool", "sent", "l0", "l1", "l2", "l3", "st"]
              + [p[4] for t in range(STEPS - 1) for p in pieces(t)]
              + ["r%s%d" % (x, m) for x in ("c", "g", "e", "o") for m in range(NR)])


def build():
    ops, part = [], ["i"]

    def op(q, n, rd, wr, fn, k=1.0, **kw):
        ops.append(dict(q=q, n=n, k=k, rd=list(rd), wr=list(wr), fn=fn, cls=(part[0], len(ops)), **kw))

    def V(n, rd, wr, fn, k=1.0):
        op("dve", n, rd, wr, fn, k)

    def S(n, rd, wr, fn, k=1.0):
        op("act", n, rd, wr, fn, k)

    def PE(cyc, rd, wr, fn):
        op("pe", cyc, rd, wr, fn)

    def val(x, T):
        return x if isinstance(x, (int, float)) else x(T)

    def ts(o, i, s1, s2, o0, o1=None):
        if o1 is None:
            return lambda g, T: g.vector.tensor_scalar(o(T), i(T), val(s1, T), None, o0)
        return lambda g, T: g.vector.tensor_scalar(o(T), i(T), val(s1, T), val(s2, T), o0, o1)

    def tt(o, i0, i1, alu):
        return lambda g, T: g.vector.tensor_tensor(o(T), i0(T), i1(T), alu)

    def cp(o, i):
        return lambda g, T: g.vector.tensor_copy(o(T), i(T))

    def act(o, i, f, **kw):
        return lambda g, T: g.scalar.activation(o(T), i(T), f, **{k: val(x, T) for k, x in kw.items()})

    def B(name, a=None, b=None, c=None):
        return lambda T: T[name][:, a:b:c] if c else T[name][:, a:b]

    def G(name, w, lst, a, b):
        return lambda T: T[name][:, 0:w].indirect(T[lst][:, a:b])

    def mms(lst):
        def fn(g, T):
            r = None
            for o, l, rh, st, sp in lst:
                r = g.tensor.matmul(o(T), l(T), rh(T), st, sp)
            return r
        return fn

    def tracks(out, w, rhs, first, last):
        return mms([(out, B(w, 15 - j, 143 - j), rhs(j), first and j == 0, last and j == 15) for j in range(16)])

    def col(j):
        return B("cf", j, j + 1)

    def dma(sem, nbytes, rd, wr, fn):
        op("sync", nbytes, rd, wr, fn, sem=sem, inc=16)

    def iota(o, pat):
        return lambda g, T: g.iota(o(T), pat, 0, 0, allow_small_or_imprecise_dtypes=True)

    def select(o, i, pat, cmp, cm):
        return lambda g, T: g.affine_select(o(T), i(T), pat, cmp, 0.0, 0, cm)

    def send(kind, key, rd, arr, nbytes, ways=None, fold=1):
        op("pool", nbytes, rd, [], None, send=(kind, key), arr=arr, ways=ways or {s: "D" for s in arr.values()}, fold=fold)

    def quarters(name, c0, c1):
        return ["%s%d" % (name, q) for q in range(c0 // 14, (c1 + 13) // 14)]

    def over(t):
        return 16 * (t % 2)

    def kept(t):
        return t < STEPS - 2 and all(c[3] in "vw" for c in CH[t])

    XA = quarters("X0", 0, 56) + quarters("X1", 0, 56) + ["Xm"]
    AA = quarters("arg0", 0, 56) + quarters("arg1", 0, 56) + ["argd"]
    DA = ["D00", "D01", "D10", "D11"]
    ET = ["E%d" % j for j in range(4)]

    dma("l0", 0, [], ["posi"], lambda g, T: g.sync.dma_start(T.posi[:], T.pos[:]))
    dma("l1", 460e3, [], ["rawc"], lambda g, T: g.sync.dma_start(T.rawc[:], T.ctl[:]))
    dma("l2", 460e3, [], ["rawx"], lambda g, T: g.sync.dma_start(T.rawx[:, 0:L], T.tape[:]))
    dma("l3", 0, [], ["thi"], lambda g, T: g.sync.dma_start(T.thi[0:8, :], T.th[:]))

    op("pool", 1, [], ["ci0"], lambda g, T: g.iota(T.ci[:, 0:1], [[0, 1]], 0, 1))
    op("pool", 256, [], ["xr"], iota(B("xr"), [[0, 2], [1, 128]]))
    op("pool", 256, [], ["xe"], iota(B("xe"), [[1, 2], [16, 8], [0, 16]]))
    for j, msk in enumerate((112, 15, 119, 8)):
        V(1, ["ci0"], ["ci%d" % (j + 1)], ts(B("ci", j + 1, j + 2), B("ci", 0, 1), msk, None, A.bitwise_and))
    V(5, ["ci%d" % j for j in range(5)], ["cf"], cp(B("cf", 0, 5), B("ci", 0, 5)))
    V(1, ["cf"], ["cf5"], ts(col(5), col(1), 15.0, None, A.add))
    V(1, ["cf"], ["cf8"], ts(col(8), col(0), 16.0, None, A.mult))
    V(256, ["cf", "xr"], ["Wi"], ts(B("Wi"), B("xr"), col(0), None, A.is_equal))
    S(256, ["Wi"], ["Wz"], act(B("Wz"), B("Wi"), F.Copy, scale=0.6))
    S(128, ["Wi"], ["Ib"], act(B("Ib"), B("Wi", 0, 128), F.Copy))
    S(128, ["Wi"], ["Iw"], act(B("Iw"), B("Wi", 0, 128), F.Copy, scale=-L / 2))
    V(144, ["cf5", "xr"], ["Wh"], ts(B("Wh"), B("xr", 0, 144), col(5), 0.5, A.is_equal, A.mult))
    S(144, ["Wh"], ["W2"], act(B("W2"), B("Wh"), F.Copy, scale=0.25))
    S(144, ["Wh"], ["Wn"], act(B("Wn"), B("Wh"), F.Copy, scale=-1.0))
    V(1, ["cf"], ["cf6"], ts(col(6), col(4), 0.0, None, A.is_equal))
    V(1, ["cf"], ["cf7"], ts(col(7), col(4), 8.0, None, A.is_equal))
    for j in range(4):
        V(256, ["cf", "xe"], [ET[j]], ts(B("E", 256 * j, 256 * j + 256), B("xe"), 2.0 * j, col(3), A.add, A.is_equal), 0.5)
    V(128, ["cf", "xe"], ["Bm"], ts(B("Bm"), B("xe", 0, 128), col(1), 0.5, A.is_equal, A.mult), 0.5)
    op("pool", 128, ["Bm"], ["Lm"], select(B("Lm"), B("Bm"), [[1, 128]], A.is_ge, -1))
    op("pool", 128, ["Bm"], ["Um"], select(B("Um"), B("Bm"), [[-1, 128]], A.is_gt, 1))
    V(128, ["cf8", "xe"], ["sel"], ts(B("sel"), B("xe", 0, 128), col(8), None, A.is_equal), 0.5)
    V(6, ["cf", "xr"], ["kcol"], ts(B("kcol", 0, 6), B("xr", 0, 96, 16), col(2), 0.5, A.add, A.add))
    S(6, ["kcol"], ["kcol2"], act(B("kcol", 6, 12), B("kcol", 0, 6), F.Copy))
    V(124, ["xr"], ["keep"], ts(B("keep", 0, 2 * LC), B("xr", 0, 2 * LC), float(LC), None, A.not_equal))
    S(LC + 1, ["xr"], ["cut"], act(B("cut", 0, LC + 1), B("xr", 0, LC + 1), F.Sign, bias=-0.5))
    S(124, ["xr"], ["c8"], act(B("c8", 0, 2 * LC), B("xr", 0, 2 * LC), F.Copy, scale=0.0, bias=8.0))
    S(192, ["xr"], ["Dd"], act(B("D", L, SRC), B("xr", 0, SRC - L), F.Copy, scale=0.0))
    S(1500, ["xr"], ["argd"], act(B("arg", L, SRC), B("xr", 0, SRC - L), F.Tanh))
    op("pool", L, [], quarters("arg1", 0, 56) + quarters("arg0", 0, 56), iota(B("arg", 0, L), [[0, L]]))
    op("pool", SRC - L, [], ["Xd", "Xm"], iota(B("X", L, SRC), [[0, SRC - L]]))
    V(4, ["thi"], ["thb"], lambda g, T: g.vector.tensor_copy(T.thb[0:8, :], T.thi[0:8, :]))
    PE(64, ["thb", "sel"], ["pR"], lambda g, T: g.tensor.matmul(T.pR[:, 0:4], T.sel[0:8, :], T.thb[0:8, :], True, True))
    V(4, ["pR"], ["thc"], ts(B("thc"), B("pR", 0, 4), -1.0, 128.5, A.mult, A.add))
    V(1, ["rawx"], ["rawm"], cp(B("rawx", L, L + 1), B("rawx", 0, 1)))
    V(K, ["rawc"], ["D10", "D11"], ts(B("D", 1, L, 2), B("rawc", 1, L, 2), 0.125, -1.0, A.mult, A.add), 0.5)
    S(128, ["Wi"], ["I8"], act(B("I8"), B("Wi", 0, 128), F.Copy, scale=0.125))
    op("pool", K, ["rawx"], quarters("X1", 0, 56), select(B("X", 1, L, 2), B("rawx", 1, L, 2), [[0, K]], A.is_ge, 0))
    V(56, ["posi"], ["P"], ts(B("P"), B("posi"), 0.0625, -0.46875, A.mult, A.add))

    wrapped = (B("pS", 64, 120), "pS")

    def drift(t):
        return 8.0 * (t + (t > 0)) - L / 2 * (t // 2)

    def lists(t):
        o = 56 * t
        src, tok = (B("pS", 0, 56), "pS") if t % 2 else wrapped if t else (B("P"), "P")
        V(56, [tok], ["offv%d" % t], ts(B("offv", o, o + 56), src, drift(t), None, A.add))
        V(56, ["offv%d" % t], ["offw%d" % t], ts(B("offw", o, o + 56), B("offv", o, o + 56), 1.0, None, A.add))
        V(56, ["offv%d" % t], ["vf"], ts(B("vf"), B("offv", o, o + 56), -drift(t) - 0.46875, None, A.add))
        if t % 2:
            src, tok = B("P"), "P"
        V(56, ["vf", tok], ["phi%d" % t], tt(B("phi", o, o + 56), src, B("vf"), A.subtract))
        for j in range(2):
            S(56, ["phi%d" % t, "cf%d" % (6 + j)], ["phm%d_%d" % (t, j)],
              act(B("phm", 2 * o + j, 2 * o + 112, 2), B("phi", o, o + 56), F.Copy, scale=col(6 + j)))

    def cstep(t):
        par, o = t % 2, 56 * t
        razor = par and t < STEPS - 1
        back = [(B("pS", 0, 56), B("Iw"), B("wr"), False, False)] * (t > 0 and not par)
        PE(256 + 64 * len(back), ["Wi", "P"] + ["Iw", "wr"] * len(back), ["pS"], mms([(B("pS", 0, 56), B("Wi", 0, 128), B("P"), True, False)] + back))
        for h in range(2):
            w, old, tok = ("Ib", "D", "D%d%d" % (par, h)) if t else ("I8", "rawc", "rawc")
            PE(H, [w, tok], ["pT%d" % h], mms([(B("pT%d" % h, 0, H), B(w), B(old, par + K * h, K * (h + 1), 2), True, False)]))
        for h in range(2):
            out, w = B("cg", H * h, H * h + H), G("D" if t else "rawc", L + over(t), "offv", o + 28 * h, o + 28 * h + 28)
            rd = (DA if t else ["rawc"]) + ["offv%d" % t] + ["Dd"] * par
            if CG[t][h] == "a":
                S(H, rd, ["cg%d" % h], act(out, w, F.Copy) if t else act(out, w, F.Copy, scale=0.125, bias=-2.0), "g")
            else:
                V(H, rd, ["cg%d" % h], cp(out, w) if t else ts(out, w, 0.125, -2.0, A.mult, A.add), "g")
        for h in range(2):
            PE(H, ["Ib", "cg%d" % h], ["pT%d" % h], mms([(B("pT%d" % h, 0, H), B("Ib"), B("cg", H * h, H * h + H), False, True)]))
        PE(1024, ["Wh", "cg0", "cg1"], ["pS"], tracks(B("pS", 0, 56), "Wh", lambda j: B("cg", j, K, 16), False, True))
        if razor:
            PE(1024, ["Wh", "D10", "D11"], ["pR"], tracks(B("pR", 0, 56), "Wh", lambda j: B("D", 1 + 2 * j, L, 32), True, False))
            PE(1024, ["Wh", "cg0", "cg1"], ["pR"], tracks(B("pR", 0, 56), "Wh", lambda j: B("cg", j, K, 16), False, False))
        for h in range(2):
            pt, sh, out = B("pT%d" % h, 0, H), B("sg", H * h, H * h + H), B("D", par + K * h, K * (h + 1), 2)
            S(H, ["pT%d" % h], ["sg%d" % h], act(sh, pt, F.Sign, bias=0.0625))
            V(H, ["pT%d" % h, "sg%d" % h], ["D%d%d" % (par, h)], tt(out, pt, sh, A.subtract))
        if razor:
            PE(1024, ["Wn", "sg0", "sg1"], ["pR"], tracks(B("pR", 0, 56), "Wn", lambda j: B("sg", j, K, 16), False, True))
        if par:
            S(56, ["pS"], ["wr"], act(B("wr"), B("pS", 0, 56), F.Sign, bias=drift(t) + 8.5 - L))
            S(56, ["pS"], ["P"], act(B("P"), B("pS", 0, 56), F.Copy))
            PE(320, ["Wi", "Iw", "wr", "P"], ["pS"], mms([(wrapped[0], B("Wi", 0, 128), B("P"), True, False), (wrapped[0], B("Iw"), B("wr"), False, True)]))
        else:
            S(56, ["pS"], ["P"], act(B("P"), B("pS", 0, 56), F.Copy))
            S(16, ["D00", "D10"], ["Dd"], act(B("D", L, L + 16), B("D", 0, 16), F.Copy))
        if t + 1 < STEPS:
            lists(t + 1)

    def crazor(m):
        o, b = 12 * m, PC * m
        tot, dl = B("pR", 64, 64 + LC), B("pR", 64 + LC, 64 + 2 * LC)
        now, bef = B("cut", 1, LC + 1), B("cut", 0, LC)
        S(56, ["pR", "thc"], ["cut"], act(B("cut", 1, 57), B("pR", 0, 56), F.Sign, bias=B("thc", m, m + 1), scale=16.0))
        PE(320, ["cut", "Bm", "Lm", "Um", "c8", "Ib"], ["pR"],
           mms([(B("pR", 64, 64 + 2 * LC), B("Ib"), B("c8", 0, 2 * LC), True, False), (tot, B("Bm"), now, False, False),
                (dl, B("Lm"), now, False, False), (dl, B("Um"), bef, False, True)]))
        V(2 * LC, ["pR", "keep"], ["cum"], lambda g, T: g.vector.tensor_tensor_scan(
            T.cum[:, 2:2 + 2 * LC], T.keep[:, 0:2 * LC], T.pR[:, 64:64 + 2 * LC], 0.0, A.mult, A.add))
        for j in range(6):
            S(85, ["cum", "kcol"], ["acc%d" % j], act(B("junk", 64 * j, 64 * j + LC - 1), B("cum", 2, LC + 1), F.Sign, bias=B("kcol", j, j + 1),
                                                      scale=-1.0, accum_out=B("acc", j, j + 1)))
        ac = ["acc%d" % j for j in range(6)]
        V(6, ac, ["colk"], ts(B("colk"), B("acc"), 0.5, (LC - 1) / 2, A.mult, A.add))
        V(96, ["cum", "colk", "xr"], ["fl"],
          tt(B("fl"), lambda T: T.cum[:, 64:64 + LC].indirect(T.colk[:, 0:6]), B("xr", 0, 96), A.is_le), "t")
        R = B("pR", 192, 198)
        PE(256, ac + ["Wi"], ["pR"], mms([(R, B("Wi", 0, 128), B("acc"), True, False)]))
        PE(1024, ["W2", "fl"], ["pR"], tracks(R, "W2", lambda j: B("fl", j, 96, 16), False, True))
        u = GATE / 2
        for j in range(2):
            S(6, ["pR"], ["own%d" % j], act(B("own", 6 * j, 6 * j + 6), R, F.Copy, scale=16.0 / u, bias=(16.0 * (LC - 1) + j) / u + 1.0))
        V(12, ["own0", "own1"], ["src%d_0" % m, "src%d_1" % m], ts(B("srcl", o, o + 12), B("own"), u, -u, A.mult, A.add))
        S(192, DA + ["Dd", "src%d_0" % m, "src%d_1" % m], ["pc%d" % m], act(B("pc", b, b + 192), G("D", SRC, "srcl", o, o + 12), F.Copy), "g")
        S(12, ["cum", "kcol", "kcol2"], ["pg%d" % m], act(B("pc", b + 192, b + PW), B("kcol"), F.Sign, bias=B("cum", 57, 58), scale=-1.0))
        send("c", (b + 192, 12, "rg%d" % m), ["pg%d" % m], {"lg%d" % m: "rg%d" % m}, 256 * 12)
        send("c", (b, 192, "rc%d" % m), ["pc%d" % m], {"lc%d" % m: "rc%d" % m}, 256 * 192)
        V(12, ["own0", "own1", "lg%d" % m], ["y12"], tt(B("y12"), B("own"), B("lc", b + 192, b + PW), A.subtract))
        V(12, ["y12"], ["dst%d" % m], ts(B("dstl", o, o + 12), B("y12"), u, None, A.mult))
        V(192, ["dst%d" % m, "lc%d" % m], DA + ["Dd"], cp(G("D", XW, "dstl", o, o + 12), B("lc", b, b + 192)), "s")

    def xtake(m, j):
        o, b, x = 12 * m + 6 * j, 192 * m + 96 * j, "eo"[j]
        if kept(2 * m + j):
            S(96, AA + ["src%d_%d" % (m, j)], ["px%s%d" % (x, m)], act(B("px", b, b + 96), G("arg", SRC, "srcl", o, o + 6), F.Copy, scale=0.625), "g")
        else:
            S(96, XA + ["Xd", "src%d_%d" % (m, j)], ["px%s%d" % (x, m)], act(B("px", b, b + 96), G("X", SRC, "srcl", o, o + 6), F.Copy), "g")
        send("x", (b, 96, "r%s%d" % (x, m)), ["px%s%d" % (x, m)], {"lx%s%d" % (x, m): "r%s%d" % (x, m)}, 512 * 96)

    def xput(m, j):
        o, b = 12 * m + 6 * j, 192 * m + 96 * j
        rd, out = ["dst%d" % m, "lx%s%d" % ("eo"[j], m)], G("X", XW, "dstl", o, o + 6)
        if kept(2 * m + j):
            S(96, rd, XA + ["Xd"], act(out, B("lx", b, b + 96), F.Tanh), "s")
        else:
            V(96, rd, XA + ["Xd"], cp(out, B("lx", b, b + 96)), "s")
        if j == 0:
            S(1, ["X00"], ["Xm"], act(B("X", L, L + 1), B("X", 0, 1), F.Copy))

    def xstep(t):
        par, o = t % 2, 56 * t
        win, wt = ("rawx", ["rawx", "rawm"]) if t == 0 else ("X", XA)
        razor = par and t < STEPS - 1
        if razor:
            xtake(t // 2, 0)
        for b in range(2):
            e = "pE%d" % b
            PE(512, ET + ["phm%d_0" % t, "phm%d_1" % t], [e],
               mms([(B(e, j, H, 8), B("E", 128 * j, 128 * j + 128), B("phm", 2 * o + 56 * b, 2 * o + 56 * b + 56), True, True) for j in range(8)]))
        for h, (c0, c1, bank, mode, _ways) in enumerate(CH[t]):
            n, j0 = 16 * (c1 - c0), 16 * c0
            e, s0 = "pE%d" % (c0 // 28), K * t + j0
            ah, dh, sh, eh = B("a", s0, s0 + n), B("d", j0, j0 + n), B("s", s0, s0 + n), B(e, j0 % H, j0 % H + n)
            at, st, dt = "a%d_%d" % (t, h), "s%d_%d" % (t, h), quarters("d", c0, c1)
            S(n, wt + ["offv%d" % t], [at], act(ah, G(win, L + over(t), "offv", o + c0, o + c1), F.Copy), "g")
            V(n, wt + ["offw%d" % t, at], dt, tt(dh, G(win, L + over(t) + 1, "offw", o + c0, o + c1), ah, A.subtract), "t")
            if mode in "wf":
                V(n, dt + [e], [st], tt(sh, dh, eh, A.mult))
            else:
                V(n, dt + [e], [e], tt(eh, dh, eh, A.mult))
                V(n, [at, e], [st], tt(sh, ah, eh, A.add))
            if t + 1 < STEPS:
                ps = [p for p in pieces(t) if p[0] == h]
                send("z", (t, h), [st] + [at] * (mode == "w"), {p[4]: p[4] for p in ps}, 512 * ps[0][3], {p[4]: p[1] for p in ps},
                     2 if mode == "w" else 1)
        for h, (c0, c1, bank, mode, _ways) in enumerate(CH[t]):
            n, j0 = 16 * (c1 - c0), 16 * c0
            pa, s0 = "pA%d" % bank, K * t + j0
            sh, ph, out = B("s", s0, s0 + n), B(pa, 0, n), B("X", par + 2 * j0, 2 * (j0 + n), 2)
            at, st, xt = "a%d_%d" % (t, h), "s%d_%d" % (t, h), quarters("X%d" % par, c0, c1)
            own = mode in "wpf"
            terms = [(["Wi", at], ph, B("Wi", 0, 128), B("a", s0, s0 + n), n) if mode in "wf" else (["Wi", st], ph, B("Wi", 0, 128), sh, n)] * own
            if t:
                r = 16 * (t % 8)
                ps = [(max(p[2], j0), min(p[2] + p[3], j0 + n), p[4]) for p in pieces(t - 1)]
                ps = [p for p in ps if p[0] < p[1]]
                if own and not ZLAST[par]:
                    terms = [(["Wz"] + [p[2] for p in ps], ph, B("Wz", r, r + 128), B("zl", s0 - K, s0 - K + n), n)] + terms
                else:
                    terms = terms + [(["Wz", z], B(pa, a - j0, b - j0), B("Wz", r, r + 128),
                                      B("zl", K * (t - 1) + a, K * (t - 1) + b), b - a) for a, b, z in ps]
            if mode == "f":
                terms = terms + [(["Wi", st], ph, B("Wi", 0, 128), sh, n)]
            for i, (rd, po, lt, rh, w) in enumerate(terms):
                if t % 8 == 0 and mode == "u":
                    S(w, rd[1:], [pa], act(po, rh, F.Copy, scale=0.6))
                else:
                    PE(4 * w, rd, [pa], mms([(po, lt, rh, i == 0 or not own, i == len(terms) - 1 or not own)]))
            src, tok = ph, [pa]
            if kept(t):
                src, tok = B("arg", par + 2 * j0, 2 * (j0 + n), 2), quarters("arg%d" % par, c0, c1)
            if mode == "s":
                src, tok = sh, [st]
            elif mode not in "pf":
                V(n, [st, pa], tok, tt(src, sh, ph, A.add))
            S(n, tok, xt, act(out, src, F.Tanh, scale=0.625))
            if par == 0 and c0 == 0:
                S(17, ["X00", "X10"], ["Xm"], act(B("X", L, L + 17), B("X", 0, 17), F.Copy))
            if t == STEPS - 1:
                dma("st", 1024 * n, quarters("X0", c0, c1) + xt, [],
                    lambda g, T, j0=j0, n=n: g.sync.dma_start(T.yx[:, 2 * j0:2 * (j0 + n)], T.X[:, 2 * j0:2 * (j0 + n)]))
        if razor:
            xtake(t // 2, 1)
            xput(t // 2, 0)
            xput(t // 2, 1)

    lists(0)
    for t in range(STEPS):
        part[0] = "c%d" % t
        cstep(t)
        if t % 2 == 1 and t < STEPS - 1:
            part[0] = "cr%d" % t
            crazor(t // 2)
    part[0] = "e"
    for p in range(2):
        PE(1024, ["Wh"] + DA[2 * p:2 * p + 2], ["pR"],
           tracks(B("pR", p, 112, 2), "Wh", lambda j, p=p: B("D", 112 * j + p, 112 * j + 112, 2), True, True))
    V(112, ["pR"], ["ycf"], ts(B("ycf"), B("pR", 0, 112), 16.0, 128.0, A.mult, A.add))
    dma("st", 0, ["ycf"], [], lambda g, T: g.sync.dma_start(T.yc[:], T.ycf[:]))
    V(56, [wrapped[1]], ["Pi"], ts(B("Pi"), wrapped[0], 16.0, 16.0 * drift(STEPS) + 7.5, A.mult, A.add))
    V(56, ["Pi"], ["yp0"], ts(B("ypi", 0, 56), B("Pi"), 8, None, A.arith_shift_right))
    V(56, ["Pi"], ["yp1"], ts(B("ypi", 56, 112), B("Pi"), 255, None, A.bitwise_and))
    V(112, ["yp0", "yp1"], ["ypf"], cp(B("ypf"), B("ypi")))
    dma("st", 0, ["ypf"], [], lambda g, T: g.sync.dma_start(T.yp[:], T.ypf[:]))
    for t in range(STEPS):
        part[0] = "x%d" % t
        xstep(t)
    return ops


def depend(ops):
    lastw, readers, arrival = {}, {}, {}
    for i, o in enumerate(ops):
        dep, arr = set(), []
        for k in o["rd"]:
            if k in arrival:
                arr.append(arrival[k])
            elif k in lastw:
                dep.add(lastw[k])
            if k in BANKS:
                dep.update(j for j in readers.get(k, []) if ops[j]["q"] != o["q"])
        for k in o["wr"]:
            if k in lastw:
                dep.add(lastw[k])
            dep.update(readers.get(k, []))
        dep.discard(i)
        for k in o["rd"]:
            readers.setdefault(k, []).append(i)
        for k in o["wr"]:
            lastw[k] = i
            readers[k] = []
        for k, sem in o.get("arr", {}).items():
            arrival[k] = (i, sem)
        o["dep"], o["wait_arr"] = sorted(dep), arr


def plain(tok):
    head = tok.rstrip("0123456789")
    if head == "arg":
        return head + tok[-1]
    if head in ("X", "D", "cf", "pE", "pA", "pT", "cg", "sg", "d", "acc", "own", "E", "ci", "yp", "W", "c", "I"):
        return tok
    i = [j for j, c in enumerate(tok + "0") if c.isdigit()][0]
    return tok[:i] + tok[i:].lstrip("0123456789")


def arrange(ops):
    place, seen, queues = {}, {}, {q: [] for q in ORDER}
    for q, text in ORDER.items():
        for r, w in enumerate(text.split()):
            name, _, back = w.partition("@")
            place[q, name] = (int(back or 0), r)
    for i, o in enumerate(ops):
        p = o["cls"][0]
        rnd = {"i": 0, "e": NR}[p] if p in ("i", "e") else int(p[-1]) // 2
        if p[0] in "cx":
            p = "r" if p[1] == "r" else p[0] + "eo"[int(p[-1]) % 2]
            p = p if p == "r" or 0 < rnd < NR else p + "0" if rnd == 0 else p.upper()
        if "send" in o:
            name = "send" + o["send"][0] + plain(o["rd"][0])
        elif not o["wr"]:
            name = "st" + plain(o["rd"][0])
        else:
            name = plain(o["wr"][0]) + ("<" + ("E" if o["rd"][1][0] == "E" else plain(o["rd"][1])) if o["q"] == "pe" else "")
        name = p + "." + name
        seen[o["q"], name, rnd] = seen.get((o["q"], name, rnd), -1) + 1
        back, r = place[o["q"], name + "'" * seen[o["q"], name, rnd]]
        queues[o["q"]].append((rnd + back, r, i))
    queues = [sorted(v, reverse=True) for v in queues.values()]
    seq, done = [], set()
    while len(seq) < len(ops):
        for v in queues:
            while v and all(j in done for j in ops[v[-1][2]]["dep"] + [x[0] for x in ops[v[-1][2]]["wait_arr"]]):
                seq.append(v.pop()[2])
                done.add(seq[-1])
    return seq


def helpers(T, topo):
    place = lambda c: (topo.host(c), topo.chip(c))
    busy = set(place(c) for c in T.cores)
    used, out = set(), {}
    names = sorted(set(w for v in CH[:-1] for c in v for w in c[4] if w != "D"))
    n = len(T.cores)
    for w in names:
        for r, c in enumerate(T.cores):
            d = T.cores[(r + 1) % n]
            if w[0] == "A":
                cand = [x for x in topo.cores_of(c) if topo.die(x) != topo.die(c) and topo.may_write(x, d)]
                out[r, w] = cand[int(w[1:]) % len(cand)]
            else:
                cand = [x for x in range(WORLD) if place(x) not in busy and topo.same_plane(c, x) and topo.die(x) == topo.die(c)
                        and topo.may_write(x, d) and place(x) not in used]
                cand.sort(key=lambda x: topo.host(x) != topo.host(c))
                out[r, w] = cand[0]
                used.add(place(cand[0]))
    return out


def bits(es):
    return sum(1 << e for e in es)


def hop_engines(T, topo, hp, r, t, p):
    c = T.cores[r]
    far = topo.engines(c, T.cores[(r + 1) % len(T.cores)])
    mine = [x for x in pieces(t) if x[0] == p[0] and (x[1][0] == "A") == (p[1][0] == "A")]
    pool = far if p[1][0] != "A" else [e for e in topo.engines(c, hp[r, p[1]]) if e not in far]
    k = len(pool) // len(mine)
    i = mine.index(p)
    return pool[i * k:(i + 1) * k]


PLAN = {}


def rank_program(g, core, T, topo):
    rank = T.rank_of(core)
    n = len(T.cores)
    if "seq" not in PLAN:
        PLAN["ops"] = build()
        depend(PLAN["ops"])
        PLAN["seq"] = arrange(PLAN["ops"])
        PLAN["help"] = helpers(T, topo)
    ops, hp = PLAN["ops"], PLAN["help"]
    if rank is None:
        sent = 0
        for (r, w), c in hp.items():
            if c != core:
                continue
            d = T.cores[(r + 1) % n]
            rid, pid = topo.addr(d, core)
            for t in range(STEPS - 1):
                for p in pieces(t):
                    if p[1] == w:
                        ap = T.zl[:, K * t + p[2]:K * t + p[2] + p[3]]
                        g.wait_ge(T.sem[p[4]], len(hop_engines(T, topo, hp, r, t, p)))
                        g.remote_dma(ap, ap, T.sem[p[4]], T.sem.sent, pid, rid, topo.mask(core, d))
                        sent += len(topo.engines(core, d))
        if sent:
            g.wait_ge(T.sem.sent, sent)
        return
    nxt, prv = T.cores[(rank + 1) % n], (rank - 1) % n
    Q = {"pool": g, "pe": g.tensor, "dve": g.vector, "act": g.scalar, "sync": g.sync}
    known = {q: {} for q in Q}
    count, clock, sent = {}, {}, [0]
    far = topo.engines(core, nxt)

    def arrives(sem):
        for t in range(STEPS - 1):
            for p in pieces(t):
                if p[4] == sem:
                    if p[1] == "D":
                        return len(hop_engines(T, topo, hp, prv, t, p))
                    return len(topo.engines(hp[prv, p[1]], core))
        return len(topo.engines(T.cores[prv], core))

    def wait(q, sem, val, more):
        if known[q].get(sem, 0) < val:
            Q[q].wait_ge(T.sem[sem], val)
            known[q][sem] = val
            for k, v in more.items():
                known[q][k] = max(known[q].get(k, 0), v)

    def remote(kind, key):
        if kind != "z":
            (rid, pid), (b, w, sem) = topo.addr(nxt, core), key
            g.remote_dma(T["l" + kind][:, b:b + w], T["p" + kind][:, b:b + w], T.sem[sem], T.sem.sent, pid, rid, bits(far))
            sent[0] += len(far)
            return
        t, h = key
        trs = []
        for p in pieces(t):
            if p[0] == h:
                rid, pid = topo.addr(nxt if p[1] == "D" else hp[rank, p[1]], core)
                es = hop_engines(T, topo, hp, rank, t, p)
                a, b = K * t + p[2], K * t + p[2] + p[3]
                how = dict(src=T.s[:, a:b], dst=T.zl[:, a:b])
                if CH[t][h][3] == "w":
                    how = dict(srcs=[T.a[:, a:b], T.s[:, a:b]], dsts=[T.zl[:, a:b]], alu_op=1)
                trs.append(RemoteDMATransfer(dst_ids=[DstId(rid=rid, pnc=pid)], dma_engine_mask=bits(es), remote_sem=T.sem[p[4]], **how))
                sent[0] += len(es)
        g.remote_dma_fused(trs, local_sem=T.sem.sent)

    at = {i: r for r, i in enumerate(PLAN["seq"])}
    for i in PLAN["seq"]:
        o = ops[i]
        q = o["q"]
        need = [j for j in o["dep"] if not (q == "pe" and ops[j]["q"] == "pe")]
        for j in sorted(need, key=lambda j: -at[j]):
            wait(q, *clock[j])
        for _j, sem in o["wait_arr"]:
            wait(q, sem, arrives(sem), {})
        if "send" in o:
            remote(*o["send"])
            continue
        sem, inc = o.get("sem", q), o.get("inc", 1)
        o["fn"](g, T).then_inc(T.sem[sem], inc)
        count[sem] = count.get(sem, 0) + inc
        clock[i] = (sem, count[sem], dict(known[q]))
    for sem, val in count.items():
        wait("pool", sem, val, {})
    g.wait_ge(T.sem.sent, sent[0])
